import numpy as np, ml_dtypes
CORES = [3,11,19,27,35,43,51,59]
N = 8
import mx_ref
BF = ml_dtypes.bfloat16
def gentries(a):
    return np.ascontiguousarray(a.reshape(8, 16, -1).transpose(0, 2, 1)).reshape(8, -1)
def gtable(e):
    e = np.asarray(e); return np.ascontiguousarray(e.reshape(8, -1, 16).transpose(0, 2, 1)).reshape(128, -1).astype(np.int32)
def gcols(t, e):
    v = np.concatenate([t.reshape(8, 16, -1, 4), np.zeros((8, 16, 1, 4), BF)], axis=2)
    return np.ascontiguousarray(np.stack([v[g][:, e[g]] for g in range(8)])).reshape(128, -1)
def tile(rs):
    return np.stack(rs, axis=2).reshape(128, -1).astype(BF)
def pick(q, e):
    c = np.concatenate([q[0].reshape(128, -1, 4), np.zeros((128, 1, 4), np.uint8)], axis=1); s = np.concatenate([q[1], np.ones((16, 1), np.uint8)], axis=1)
    return (np.ascontiguousarray(c[:, e].reshape(128, -1)), np.ascontiguousarray(s[:, e]))
def join(*qs):
    return (np.concatenate([q[0] for q in qs], axis=1), np.concatenate([q[1] for q in qs], axis=1))
def put(q, e, v):
    c, s = q[0].reshape(128, -1, 4).copy(), q[1].copy(); c[:, e] = v[0].reshape(128, -1, 4); s[:, e] = v[1]
    return (c.reshape(128, -1), s)
def pk(c, s):
    return (np.ascontiguousarray(c), mx_ref.live(s))
def emit(q):
    return q[0], q[1]
def packed(v, rng):
    q = [mx_ref.quantize(np.ascontiguousarray(v[r])) for r in range(N)]
    return np.stack([a for a, b in q]), np.stack([mx_ref.plane(b, rng) for a, b in q])
def values_of_codes():
    e, c = np.zeros((128, 128, 4), np.float32), np.zeros((128, 2, 4), np.uint8)
    e[np.arange(128), np.arange(128), 0] = 1
    c[:127, :, 0] = np.arange(256).reshape(2, 128).T[:127]
    return mx_ref.matmul(mx_ref.quantize(e.reshape(128, 512).astype(BF)), (c.reshape(128, 8), np.full((16, 2), 127, np.uint8))).T.reshape(-1).astype(np.float64)
CODE_VALUE, SCALE_VALUE = values_of_codes(), 2.0 ** (np.arange(256) - 127.0)
def decode(q):
    return (CODE_VALUE[q[0]].reshape(16, 8, -1, 4) * SCALE_VALUE[q[1]][:, None, :, None] + 0.0).reshape(128, -1).astype(np.float32)
def f(rng, *shape):
    return mx_ref.flush((rng.standard_normal(shape, dtype=np.float32) * np.exp2(rng.integers(-2, 3, shape[:-1] + (1,)))).astype(BF))
def wide(rng, *shape, cols=0):
    v = rng.standard_normal(shape, dtype=np.float32) * np.exp2(rng.integers(-12, 13, shape)).astype(np.float32)
    if cols: v *= np.repeat(np.exp2(rng.integers(-cols, cols + 1, shape[:-2] + (1, shape[-1] // 4))) * (rng.random(shape[:-2] + (1, shape[-1] // 4)) > 0.0625), 4, axis=-1).astype(np.float32)
    return mx_ref.flush(v.astype(BF))
C, K, A, B, R = 256, 64, 4, 4, 3
STEP = [1, 2, 4]
def classes(key):
    c, one, two = np.zeros((8, C), int), np.full((8, K), -1), np.full((8, K), -1)
    for g in range(8):
        first, mine = np.unique(key[g], return_index=True, return_inverse=True)[1:]
        low = np.sort(first)
        c[g] = np.searchsorted(low, first[mine])
        for k in range(len(low)):
            m = np.flatnonzero(c[g] == k)
            one[g, k] = m[0]
            two[g, k] = m[min(1, len(m) - 1)]
    return c, one, two
def numbers_of(rng):
    return {"x": np.array(f(rng, N, 128, 4 * C)), "u": np.array(f(rng, N, 128, 512)), "v": np.array(f(rng, N, 128, 512))}
def lists_of(rng):
    return {"nx": rng.integers(0, C, (N, 8, C)), "co": rng.integers(0, K, (N, 8, C))}
def stored(l):
    return {k: np.stack([gtable(e) for e in l[k]]) for k in ("nx", "co")}
def weights(rng, w):
    c, p = packed(w, rng)
    return {"wc": c, "ws": p}
def quiet(rng):
    w = np.array(f(rng, N, 128, 2048)).reshape(N, 8, 16, 4, 8, 16, 4)
    w[:, :, :8] = 0
    w[:, :, :, :, :, :8] = 0
    return weights(rng, w.reshape(N, 128, 2048))
def marked(d, m, k):
    x = d["x"].reshape(N, 8, 16, C, 4)
    u = d["u"].reshape(N, 128, 128, 4)
    x[:, :, :8] = 0
    k = k.astype(np.float32)
    for i in range(2):
        x[:, :, i, :, :2] = m[:, :, :, i].astype(np.float32).astype(BF)
        u[:, :, i::16] = 0
        for h in range(i, 128, 16):
            u[:, h, h, 0] = k.astype(BF)
            u[:, h, h, 1] = (-k).astype(BF)
    return {"x": x.reshape(N, 128, 4 * C), "u": u.reshape(N, 128, 512), "v": d["v"]}
def setup_inputs(rng):
    return {**numbers_of(rng), **stored(lists_of(rng)), **weights(rng, f(rng, N, 128, 2048))}
def setup_inputs_full(rng):
    d, l = numbers_of(rng), lists_of(rng)
    o = rng.permutation(N)
    bits = np.zeros((N, 8, C), int)
    for r in range(N):
        e = np.argsort(rng.random((8, C)), axis=1)
        if o[r] % 4 == 3:
            l["co"][r] = rng.integers(0, K, (8, 1))
            bits[r] = e % (1 + rng.permutation(8) % 4)[:, None]
        else:
            k, one, two = classes(np.minimum(e, K - 1) if o[r] % 4 == 1 else e % K)
            l["co"][r] = k % A + A * rng.integers(0, K // A, (8, C))
            l["nx"][r] = np.take_along_axis(one, k // A % B + B * rng.integers(0, K // B, (8, C)), axis=1)
            bits[r] = k // (A * B)
    m = np.zeros((N, 8, C, 2, 2))
    m[:, :, :, 0] = 2 * (np.arange(2) == (bits >> 1)[:, :, :, None])
    m[:, :, :, 1] = 2 * (np.arange(2) == (bits & 1)[:, :, :, None])
    return {**marked(d, m, np.ones(N)), **stored(l), **quiet(rng)}
def setup_inputs_near(rng):
    d, l = numbers_of(rng), lists_of(rng)
    p = np.array([[0, 0], [2, 2], [3, 2], [2, 3], [2, 0], [0, 2]])
    e = np.argsort(rng.random((N, 8, C)), axis=2)
    h = np.argsort(rng.random((N, 8, C)), axis=2)
    m = np.stack([p[e // 4 % 6], p[h % 6]], axis=3) * 2.0 ** np.array([-30, -12, 0, 28])[e % 4][:, :, :, None, None]
    k = np.where(rng.permutation(N) < N // 2, 2.0 ** -30, 1.0)
    return {**marked(d, m, k), **stored(l), **quiet(rng)}
def setup_inputs_lists(rng):
    d, l = numbers_of(rng), lists_of(rng)
    o = rng.permutation(N)
    x = d["x"].reshape(N, 128, C, 4)
    for r in range(N):
        a = x[r][:, :2].copy()
        if o[r] % 4 == 0: l["nx"][r] = np.arange(C)
        if o[r] % 4 == 1: l["nx"][r] = rng.integers(0, C, (8, 1))
        if o[r] % 4 == 2:
            l["nx"][r] = C - 1 - np.arange(C)
            a[:, 1] = 0
            x[r] = a[:, rng.permutation(C) % 2]
        if o[r] % 4 == 3:
            l["co"][r] = rng.integers(0, K, (8, 1))
            x[r] = a[:, np.zeros(C, int)]
    return {"x": x.reshape(N, 128, 4 * C), "u": d["u"], "v": d["v"], **stored(l), **weights(rng, f(rng, N, 128, 2048))}
def setup_inputs_huge(rng):
    d, l = numbers_of(rng), lists_of(rng)
    o = rng.permutation(N)
    c = np.stack([rng.permutation(C) % 2 * 2.0 - 1.0 for r in range(N)])
    c[o == 0] = 1
    c[o == 1] = -1
    p = rng.random((N, 128, C, 4))
    x = np.where(c[:, None, :, None] < 0, -2.0 ** 30 * (1 - 0.125 * p), 2.0 ** 28 * (1 - 0.5 * p))
    k = np.stack([rng.permutation(8) % 4 for r in range(N)])
    s = 1.0 - 2.0 * np.stack([k >> 1, k & 1], axis=2)
    u = d["u"].reshape(N, 128, 8, 16, 4)
    a = 2.0 ** 30 * (1 - 0.25 * rng.random((N, 128, 8, 2, 4))) * s[:, None, :, :, None]
    u[:, :, :, :2] = a.astype(np.float32).astype(BF)
    w = np.zeros((N, 128, 4, 128, 4), np.float32)
    i = np.arange(128)
    for b in range(4): w[:, i, b, i, b] = 8
    return {"x": x.astype(np.float32).reshape(N, 128, 4 * C).astype(BF), "u": u.reshape(N, 128, 512), "v": d["v"], **stored(l), **weights(rng, w.reshape(N, 128, 2048).astype(BF))}
def setup_inputs_spread(rng):
    d = setup_inputs(rng)
    d["x"] = wide(rng, N, 128, 4 * C, cols=6)
    return d
def check_inputs(d):
    b = []
    for k in ("x", "u", "v"):
        a = np.abs(d[k].astype(np.float32))
        if not (np.isfinite(a).all() and ((a == 0) | (a >= 2.0 ** -30) & (a <= 2.0 ** 30)).all()): b.append("a value of " + k)
    if ((d["nx"] < 0) | (d["nx"] >= C)).any(): b.append("an entry of nx")
    if ((d["co"] < 0) | (d["co"] >= K)).any(): b.append("an entry of co")
    if ((d["wc"] == 0x7F) | (d["wc"] == 0xFF)).any(): b.append("a code of wc is no number")
    for r in range(N):
        s = mx_ref.live(d["ws"][r])
        if ((s > 1) & (s < 64) | (s > 191)).any(): b.append("a scale of ws")
    return b
def reference(x, u, v, nx, co, wc, ws):
    qu = [mx_ref.quantize(u[r]) for r in range(N)]
    lay = [pk(wc[r], ws[r]) for r in range(N)]
    now = [x[r] for r in range(N)]
    to = [gentries(nx[r]).astype(np.int64) for r in range(N)]
    cl = [gentries(co[r]).astype(np.int64) for r in range(N)]
    for t in range(R):
        held, sent = [], []
        for r in range(N):
            q = mx_ref.quantize(now[r])
            held.append(decode(q).astype(BF))
            neg = mx_ref.matmul(qu[r], q) + np.float32(0.0) < 0
            key = 4 * B * (cl[r] % A) + 4 * (np.take_along_axis(cl[r], to[r], axis=1) % B) + 2 * neg[::16] + neg[1::16]
            cl[r], one, two = classes(key)
            z = (gcols(held[r], one).astype(np.float32) + gcols(held[r], two).astype(np.float32)) * np.float32(0.5)
            sent.append(mx_ref.quantize(z.astype(BF)))
        for r in range(N):
            e = (r + STEP[t]) % N
            h = tile([np.maximum(mx_ref.matmul(pick(lay[e], np.arange(128 * b, 128 * b + 128)), sent[r]), np.float32(0.0)) * np.float32(0.03125) for b in range(4)])
            came = decode(mx_ref.quantize(h)).astype(BF)
            now[r] = (held[r].astype(np.float32) + gcols(came, cl[r]).astype(np.float32)).astype(BF)
    y, ol = np.zeros((N, 128, C), np.float32), np.zeros((N, 8, C), np.float32)
    oc, osc = np.zeros((N, 128, 4 * C), np.uint8), np.zeros((N, 16, C), np.uint8)
    for r in range(N):
        q = mx_ref.quantize(now[r])
        y[r] = mx_ref.matmul(mx_ref.quantize(v[r]), q)
        ol[r] = cl[r]
        oc[r], osc[r] = emit(q)
    return {"y": y, "ol": ol, "oc": oc, "osc": osc}

@@ -1,0 +1,403 @@
+from concourse.mybir import dt, AluOpType, AxisListType, ActivationFunctionType
+
+C, K, R = 256, 64, 3
+STEP = [1, 2, 4]
+PL = C + 16
+ZL = K + 16
+REV = (2, 3)
+HOR = 256
+CODES = "float8_e4m3fn_x4"
+
+SCRATCH = {}
+for _n, _w, _d in (
+        ("ones", 512, "b"), ("strip", 516, "b"), ("zero", 512, "b"), ("eq", 512, "c"), ("esc", 512, "p"), ("ut", 512, "b"), ("qu", 128, "c"),
+        ("su", 128, "p"), ("uu", 256, "c"), ("us", 256, "p"), ("vt", 512, "b"), ("qv", 128, "c"), ("sv", 128, "p"), ("wq", 512, "c"), ("wp", 512, "p"),
+        ("nxi", 16, "i"), ("coi", 16, "i"), ("nxo", 16, "u"), ("coo", 16, "u"), ("uoi", 16, "i"), ("uoo", 16, "u"), ("iot", 272, "f"), ("pif", 1, "f"),
+        ("m4t", 64, "b"), ("pi", 4, "i"), ("p15", 4, "i"), ("p16", 4, "i"), ("si", 4, "i"), ("kap", 4, "f"), ("kv", 4, "f"),
+        ("lo", 1, "f"), ("hi", 1, "f"), ("nka", 1, "f"), ("fh", 4 * PL, "b"), ("sa", 256, "b"), ("sb", 256, "b"),
+        ("k1", 256, "b"), ("pk", 256, "b"), ("cm4", 256, "b"), ("cm16", 256, "b"), ("kr", 288, "b"), ("cr", 288, "b"), ("ta", 256, "b"),
+        ("tb", 288, "b"), ("e1", 32, "f"), ("kwf", 16, "f"), ("kw", 16, "u"), ("cw", 16, "u"), ("junk", 512, "b"), ("jun2", 256, "f"),
+        ("ww", 1024, "f"), ("acc", 4, "f"), ("fr", 64, "f"), ("lt", 65, "b"), ("f16", 4, "u"), ("s16", 4, "u"), ("r16", 4, "u"), ("o16", 4, "u"),
+        ("fi", 4, "i"), ("si2", 20, "i"), ("rr", 64, "b"), ("om", 256, "b"), ("ow", 256, "b"), ("g1", 256, "b"), ("zk", 4 * ZL, "b"),
+        ("zt", 512, "b"), ("ht", 512, "b"), ("ri", 64, "i"), ("rm", 64, "i"), ("rm4", 64, "b"), ("dh", 256, "b"), ("g2", 512, "b"), ("cf", 256, "f"),
+        ("yo", 256, "f"), ("w0", 256, "b"), ("w1", 256, "b"),
+        ("zc", 128 + R * K, "c"), ("zp", 128 + R * K, "p"), ("hc", 128 + R * K, "c"), ("hp", 128 + R * K, "p")):
+    SCRATCH[_n] = ("sbuf", [128, _w], {"b": "bfloat16", "c": CODES, "p": "uint8", "i": "int32", "u": "uint16", "f": "float32"}[_d])
+for _n in ("pf", "pw"):
+    SCRATCH[_n] = ("psum", [128, 2048], "float32")
+for _i in range(4):
+    SCRATCH["m%d" % _i] = ("sbuf", [128, 256], "bfloat16")
+    SCRATCH["t%d" % _i] = ("sbuf", [128, 1024], "bfloat16")
+    SCRATCH["q%d" % _i] = ("sbuf", [128, 256], CODES)
+    SCRATCH["s%d" % _i] = ("sbuf", [128, 256], "uint8")
+for _i in range(R):
+    for _n in "zh":
+        SCRATCH["%sq%d" % (_n, _i)] = ("sbuf", [128, 128], CODES)
+        SCRATCH["%ss%d" % (_n, _i)] = ("sbuf", [128, 128], "uint8")
+
+DMAS = ["dx0", "dx1", "du", "dv", "dwc", "dws", "dn", "dc", "dol", "dy0", "dy1", "doc0", "doc1", "ds0", "ds1", "ds2", "ds3"]
+SEMAPHORES = ["cv", "cs", "ct", "cg", "left"] + ["za%d" % i for i in range(R)] + ["ha%d" % i for i in range(R)] + DMAS
+
+
+def rank_program(g, core, T, topo):
+    rank = T.rank_of(core)
+    if rank is None:
+        return
+    add, mult, amax = AluOpType.add, AluOpType.mult, AluOpType.max
+    F = ActivationFunctionType
+    eng = {"v": g.vector, "s": g.scalar, "t": g.tensor, "g": g, "y": g.sync}
+    count = {"cv": 0, "cs": 0, "ct": 0, "cg": 0, "left": 0}
+    known = {q: {} for q in eng}
+    wrote, read = {}, {}
+
+    def over(book, reg):
+        return [e for e in book.get(reg[0], []) if e[0] < reg[2] and reg[1] < e[1]]
+
+    def need(q, reads, writes):
+        want = {}
+        for reg in reads:
+            for e in over(wrote, reg):
+                want[e[3]] = max(want.get(e[3], 0), e[4])
+            if reg[0] in ("pf", "pw"):
+                for e in over(read, reg):
+                    if e[2] != q:
+                        want[e[3]] = max(want.get(e[3], 0), e[4])
+        for reg in writes:
+            for e in over(wrote, reg):
+                want[e[3]] = max(want.get(e[3], 0), e[4])
+            for e in over(read, reg):
+                if e[2] != q:
+                    want[e[3]] = max(want.get(e[3], 0), e[4])
+        for s in sorted(want):
+            if known[q].get(s, 0) < want[s]:
+                eng[q].wait_ge(T.sem[s], want[s])
+                known[q][s] = want[s]
+
+    def note(q, reads, writes, s, n):
+        for reg in writes:
+            for book in (wrote, read):
+                book[reg[0]] = [e for e in book.get(reg[0], []) if not (reg[1] <= e[0] and e[1] <= reg[2])]
+            wrote[reg[0]].append((reg[1], reg[2], q, s, n))
+        for reg in reads:
+            book = [e for e in read.get(reg[0], []) if not (e[2] == q and reg[1] <= e[0] and e[1] <= reg[2])]
+            book.append((reg[1], reg[2], q, s, n))
+            read[reg[0]] = book
+
+    def op(q, call, reads, writes):
+        need(q, reads, writes)
+        s = "c" + q
+        count[s] += 1
+        call().then_inc(T.sem[s], 1)
+        note(q, reads, writes, s, count[s])
+
+    def dma(q, s, out, in_, reads, writes):
+        need(q, reads, writes)
+        eng[q].dma_start(out, in_).then_inc(T.sem[s], 16)
+        note(q, reads, writes, s, 16)
+
+    V, S, PE = g.vector, g.scalar, g.tensor
+
+    def r(name, a=0, b=None):
+        return (name, a, T[name].shape[1] if b is None else b)
+
+    def quant(qb, sb_, tile, a, n, c0=0):
+        if tile == "t0":
+            src = [(tile, 4 * c0, 4 * (c0 + n))]
+        elif tile in ("t1", "t2", "t3"):
+            src = [(tile, C * b + c0, C * b + c0 + n) for b in range(4)]
+        else:
+            src = [r(tile)]
+        op("v", lambda: V.quantize_mx(T[qb][:, a:a + n], T[sb_][:, a:a + n], T[tile][:, 4 * c0:4 * (c0 + n)]),
+           src, [r(qb, a, a + n), r(sb_, a, a + n)])
+
+    def fill(name, a, b, val):
+        op("v", lambda: V.memset(T[name][:, a:b], val), [], [r(name, a, b)])
+
+    def whole(name, a, b, pattern, base=0, per=0):
+        op("g", lambda: g.iota(T[name][:, a:b], pattern, base, per, allow_small_or_imprecise_dtypes=True), [], [r(name, a, b)])
+
+    def ts(out, in0, s1, s2, op0, op1, reads, writes):
+        if s2 is None:
+            op("v", lambda: V.tensor_scalar(out, in0, s1, None, op0), reads, writes)
+        else:
+            op("v", lambda: V.tensor_scalar(out, in0, s1, s2, op0, op1), reads, writes)
+
+    def tt(out, a, b, o, reads, writes):
+        op("v", lambda: V.tensor_tensor(out, a, b, o), reads, writes)
+
+    def cp(out, a, reads, writes):
+        op("v", lambda: V.tensor_copy(out, a), reads, writes)
+
+    def act(out, a, f, reads, writes, **kw):
+        op("s", lambda: S.activation(out, a, f, **kw), reads, writes)
+
+    def mm(bank, buf, n, lq, ls, la, rq, rs, ra):
+        op("t", lambda: PE.matmul_mx(T[buf][:, 512 * bank:512 * bank + n], T[lq][:, la:la + 128], T[ls][:, la:la + 128],
+                                     T[rq][:, ra:ra + n], T[rs][:, ra:ra + n], True, True),
+           [r(lq, la, la + 128), r(ls, la, la + 128), r(rq, ra, ra + n), r(rs, ra, ra + n)], [(buf, 512 * bank, 512 * bank + 512)])
+
+    def bank(buf, b):
+        return (buf, 512 * b, 512 * b + 512)
+
+    def send(kind, t, peer):
+        cq, sq = kind + "q%d" % t, kind + "s%d" % t
+        need("g", [r(cq, 0, 64), r(sq, 0, 64)], [])
+        dst = T.cores[peer]
+        rid, pid, _se = topo.addr(dst)
+        m, arr = topo.mask(core, dst), T.sem[kind + "a%d" % t]
+        a, e = 128 + K * t, 128 + K * t + K
+        g.remote_dma(T[kind + "c"][:, a:e].bitcast(dt.uint8), T[cq][:, 0:64].bitcast(dt.uint8), arr, T.sem.left, pid, rid, m)
+        g.remote_dma(T[kind + "p"][:, a:e], T[sq][:, 0:64], arr, T.sem.left, pid, rid, m)
+        count["left"] += 2 * len(topo.engines(core, dst))
+
+    def arrival(kind, t, peer):
+        n = 2 * len(topo.engines(T.cores[peer], core))
+        a, e = 128 + K * t, 128 + K * t + K
+        note("r", [], [(kind + "c", a, e), (kind + "p", a, e)], kind + "a%d" % t, n)
+
+    def as_list(row, dest, scale, base):
+        op("v", lambda: V.transpose(T.ta[:, 0:256], T[row][:, 16:272]), [r(row)], [r("ta")])
+        op("v", lambda: V.transpose(T.tb[:, 0:288], T[row][:, 0:288]), [r(row)], [r("tb")])
+        for k, (src, a, m) in enumerate((("ta", 0, "lo"), ("ta", 16, "hi"), ("tb", 16, "hi"), ("tb", 32, "lo"))):
+            end = 288 if a == 32 else 256
+            ts(T.e1[:, 8 * k:8 * k + 8], T[src][:, a:end:32], T[m][:, 0:1], None, mult, None, [r(src), r(m)], [r("e1", 8 * k, 8 * k + 8)])
+        tt(T.kwf[:, 0:16:2], T.e1[:, 0:8], T.e1[:, 16:24], add, [r("e1", 0, 8), r("e1", 16, 24)], [("kwf", 0, 8)])
+        tt(T.kwf[:, 1:16:2], T.e1[:, 8:16], T.e1[:, 24:32], add, [r("e1", 8, 16), r("e1", 24, 32)], [("kwf", 8, 16)])
+        ts(T[dest][:, 0:16], T.kwf[:, 0:16], scale, base, mult, add, [r("kwf")], [r(dest)])
+
+    def prekeys_own():
+        act(T.cm16[:, 0:256], T.cm4[:, 0:256], F.Copy, [r("cm4")], [r("cm16")], bias=2.0, scale=4.0)
+
+    def prekeys_next():
+        tt(T.pk[:, 0:256], T.cm4[:, 0:256].indirect(T.nxo[:, 0:16]), T.cm16[:, 0:256], add, [r("cm4"), r("nxo"), r("cm16")], [r("pk")])
+
+    dma("y", "du", T.ut[:], T.u[:], [], [r("ut")])
+    for h in range(2):
+        dma("y", "dx%d" % h, T.t0[:, 512 * h:512 * h + 512], T.x[:, 512 * h:512 * h + 512], [], [r("t0", 512 * h, 512 * h + 512)])
+    dma("s", "dc", T.coi[:], T.co[:], [], [r("coi")])
+    dma("s", "dn", T.nxi[:], T.nx[:], [], [r("nxi")])
+    fill("strip", 0, 516, 0.0)
+    whole("pif", 0, 1, [[0, 1]], 0, 1)
+    whole("iot", 0, 128, [[1, 128]])
+    whole("m4t", 0, 64, [[0, 16], [4, 4]])
+    whole("uoi", 0, 16, [[1, 2], [16, 8]])
+    whole("pi", 0, 4, [[0, 4]], 0, 1)
+    whole("si", 0, 4, [[16, 4]])
+    whole("ones", 0, 512, [[0, 512]], 1)
+    whole("iot", 128, 272, [[1, 144]], 128)
+    ts(T.strip[:, 3:515:4], T.iot[:, 0:128], T.pif[:, 0:1], None, AluOpType.is_equal, None, [r("iot", 0, 128), r("pif")], [r("strip", 3, 515)])
+    cp(T.uoo[:, 0:16], T.uoi[:, 0:16], [r("uoi")], [r("uoo")])
+    cp(T.coo[:, 0:16], T.coi[:, 0:16], [r("coi")], [r("coo")])
+    for b in range(4):
+        op("v", lambda: V.quantize_mx(T.eq[:, 128 * b:128 * b + 128], T.esc[:, 128 * b:128 * b + 128], T.strip[:, 3 - b:515 - b]),
+           [r("strip")], [r("eq", 128 * b, 128 * b + 128), r("esc", 128 * b, 128 * b + 128)])
+    ts(T.p15[:, 0:4], T.pi[:, 0:4], 15, None, AluOpType.bitwise_and, None, [r("pi")], [r("p15")])
+    act(T.cm4[:, 0:256], T.m4t[:, 0:64].indirect(T.coo[:, 0:16]), F.Copy, [r("m4t"), r("coo")], [r("cm4")])
+    tt(T.kap[:, 0:4], T.p15[:, 0:4], T.si[:, 0:4], add, [r("p15"), r("si")], [r("kap")])
+    cp(T.nxo[:, 0:16], T.nxi[:, 0:16], [r("nxi")], [r("nxo")])
+    quant("qu", "su", "ut", 0, 128)
+    cp(T.uu[:, 0:256].bitcast(dt.uint32), T.qu[:, 0:128].bitcast(dt.uint32).indirect(T.uoo[:, 0:16]), [r("qu"), r("uoo")], [r("uu")])
+    prekeys_own()
+    act(T.us[:, 0:256], T.su[:, 0:128].indirect(T.uoo[:, 0:16]), F.Copy, [r("su"), r("uoo")], [r("us")])
+    need("y", [r("t0")], [])
+    dma("y", "dwc", T.wq[:, 0:512].bitcast(dt.uint8), T.wc[:, 0:2048], [], [r("wq")])
+    dma("y", "dws", T.wp[:, 0:512], T.ws[:, 0:512], [], [r("wp")])
+    dma("y", "dv", T.vt[:], T.v[:], [], [r("vt")])
+    quant("q0", "s0", "t0", 0, 128, 0)
+    prekeys_next()
+    ts(T.kv[:, 0:4], T.kap[:, 0:4], 2.0, -63.0, mult, add, [r("kap")], [r("kv")])
+    ts(T.nka[:, 0:1], T.kap[:, 3:4], -256.0, None, mult, None, [r("kap")], [r("nka")])
+    quant("q0", "s0", "t0", 128, 128, 128)
+    whole("ones", HOR, HOR + 1, [[0, 1]])
+    whole("lt", 64, 65, [[0, 1]], -64)
+    for b in range(4):
+        whole("fh", PL * b + C, PL * b + PL, [[0, 16]])
+        whole("zk", ZL * b, ZL * b + 1, [[0, 1]])
+    whole("zt", 256, 512, [[0, 256]])
+    for n in ("kr", "cr"):
+        whole(n, 0, 16, [[0, 16]])
+        whole(n, 272, 288, [[0, 16]])
+
+    for t in range(R):
+        q, s = "q%d" % t, "s%d" % t
+        to, frm = (rank + STEP[t]) % len(T.cores), (rank - STEP[t]) % len(T.cores)
+        for h in range(2):
+            for k in range(2):
+                mm(2 * h + k, "pw", 128, "uu", "us", 128 * k, q, s, 128 * h)
+        for b in range(4):
+            mm(b, "pf", 256, "eq", "esc", 128 * b, q, s, 0)
+        for h, k in ((0, 0), (0, 1), (1, 0), (1, 1)):
+            n, a, e = ("sa", "sb")[k], 128 * h, 128 * h + 128
+            act(T[n][:, a:e], T.pw[:, 1024 * h + 512 * k:1024 * h + 512 * k + 128], F.Sign, [bank("pw", 2 * h + k)], [r(n, a, e)],
+                bias=-1e-36, scale=-1.0)
+        for a, e in ((0, 128), (128, 256)):
+            tt(T.k1[:, a:e], T.sa[:, a:e], T.pk[:, a:e], add, [r("sa", a, e), r("pk", a, e)], [r("k1", a, e)])
+            tt(T.kr[:, 16 + a:16 + e], T.k1[:, a:e], T.sb[:, a:e], mult, [r("k1", a, e), r("sb", a, e)], [r("kr", 16 + a, 16 + e)])
+
+        def plane_f(b):
+            act(T.fh[:, PL * b:PL * b + C], T.pf[:, 512 * b:512 * b + C], F.Copy, [bank("pf", b)], [r("fh", PL * b, PL * b + C)])
+
+        def mask(i):
+            ts(T["m%d" % i][:, 0:256], T.kr[:, 16:272], T.kv[:, i:i + 1], 2.0 ** -10, AluOpType.not_equal, amax,
+               [r("kr", 16, 272), r("kv")], [r("m%d" % i, 0, 256)])
+
+        def scan(i):
+            if i in REV:
+                op("v", lambda: V.tensor_tensor_scan(T.ww[:, 256 * i + 255:256 * i - 1:-1], T["m%d" % i][:, 255::-1],
+                                                     T.ones[:, HOR + 255:HOR - 1:-1], 1.0, mult, add),
+                   [r("m%d" % i), r("ones", HOR, HOR + 256)], [r("ww", 256 * i, 256 * i + 256)])
+            else:
+                op("v", lambda: V.tensor_tensor_scan(T["w%d" % i][:, 0:256], T["m%d" % i][:, 0:256], T.ones[:, 0:256], 1.0, mult, mult),
+                   [r("m%d" % i), r("ones", 0, 256)], [r("w%d" % i)])
+
+        def total(i):
+            act(T.junk[:, 256 * i:256 * i + 256], T["w%d" % i][:, 0:256], F.Copy, [r("w%d" % i)],
+                [r("junk", 256 * i, 256 * i + 256), r("ww", 256 * i, 256 * i + 1)], accum_out=T.ww[:, 256 * i:256 * i + 1])
+        plane_f(0)
+        plane_f(1)
+        mask(0)
+        mask(1)
+        scan(0)
+        plane_f(2)
+        total(0)
+        mask(2)
+        scan(1)
+        total(1)
+        plane_f(3)
+        mask(3)
+        scan(2)
+        scan(3)
+        vv, rv = T.ww[:, 0:1024:256], [r("ww", 256 * i, 256 * i + 1) for i in range(4)]
+        d = [T.si2[:, 4 * k:4 * k + 4] for k in range(5)]
+        e = [r("si2", 4 * k, 4 * k + 4) for k in range(5)]
+        cp(T.f16[:, 0:4], vv, rv, [r("f16")])
+        ts(d[0], vv, 1024.0, None, mult, None, rv, [e[0]])
+        ts(T.fr[:, 0:64], T.iot[:, 0:272].indirect(T.f16[:, 0:4]), 1.0 - 2.0 ** -10, None, mult, None, [r("iot"), r("f16")], [r("fr")])
+        for i in range(3):
+            act(T.jun2[:, 64 * i:64 * i + 64], T.fr[:, 0:64], F.Sign, [r("fr"), rv[i]], [r("jun2", 64 * i, 64 * i + 64), r("acc", i, i + 1)],
+                bias=T.ww[:, 256 * i:256 * i + 1], scale=-1.0, accum_out=T.acc[:, i:i + 1])
+        for b in range(4):
+            act(T.g1[:, 64 * b:64 * b + 64], T.fh[:, PL * b:PL * b + PL].indirect(T.f16[:, 0:4]), F.Copy,
+                [r("fh", PL * b, PL * b + PL), r("f16")], [r("g1", 64 * b, 64 * b + 64)])
+
+        def mean(b):
+            tt(T.zk[:, ZL * b + 1:ZL * b + 65], T.fh[:, PL * b:PL * b + PL].indirect(T.s16[:, 0:4]), T.g1[:, 64 * b:64 * b + 64], add,
+               [r("fh", PL * b, PL * b + PL), r("s16"), r("g1", 64 * b, 64 * b + 64)], [r("zk", ZL * b + 1, ZL * b + 65)])
+        ts(T.fi[:, 0:4], d[0], 10, None, AluOpType.arith_shift_right, None, [e[0]], [r("fi")])
+        ts(d[1], d[0], 1023, None, AluOpType.bitwise_and, None, [e[0]], [e[1]])
+        ts(T.lt[:, 0:64], T.fr[:, 0:64], T.ww[:, 768:769], 2.0, AluOpType.is_lt, mult, [r("fr"), rv[3]], [r("lt", 0, 64)])
+        tt(d[2], T.fi[:, 0:4], d[1], add, [r("fi"), e[1]], [e[2]])
+        op("v", lambda: V.tensor_reduce(T.acc[:, 3:4], T.lt[:, 0:65], AxisListType.X, add), [r("lt")], [r("acc", 3, 4)])
+        ts(d[3], d[2], 255, None, AluOpType.bitwise_and, None, [e[2]], [e[3]])
+        tt(d[4], d[3], T.fi[:, 0:4], amax, [e[3], r("fi")], [e[4]])
+        ts(T.r16[:, 0:4], T.acc[:, 0:4], 0.5, 31.0, mult, add, [r("acc")], [r("r16")])
+        cp(T.s16[:, 0:4], d[4], [e[4]], [r("s16")])
+        cp(T.rr[:, 0:64], T.iot[:, 0:272].indirect(T.r16[:, 0:4]), [r("iot"), r("r16")], [r("rr")])
+        mean(0)
+        for i in range(4):
+            if i < 3:
+                ts(T.om[:, 64 * i:64 * i + 64], T.rr[:, 0:64], T.kap[:, i:i + 1], 256.0, AluOpType.not_equal, mult,
+                   [r("rr"), r("kap")], [r("om", 64 * i, 64 * i + 64)])
+            else:
+                act(T.om[:, 64 * i:64 * i + 64], T.rr[:, 0:64], F.Abs, [r("rr"), r("nka")], [r("om", 64 * i, 64 * i + 64)],
+                    bias=T.nka[:, 0:1], scale=256.0)
+        mean(1)
+        op("v", lambda: V.tensor_tensor_scan(T.ow[:, 0:256], T.ones[:, 0:256], T.om[:, 0:256], 0.0, add, AluOpType.min),
+           [r("ones", 0, 256), r("om")], [r("ow")])
+        mean(2)
+        ts(T.o16[:, 0:4], T.ow[:, 63:256:64], -1.0, 64.0, mult, add, [r("ow")], [r("o16")])
+        mean(3)
+        for b in range(4):
+            o, i, rd, wr = T.zt[:, b:256:4], T.zk[:, ZL * b:ZL * b + 65].indirect(T.o16[:, 0:4]), \
+                [r("zk", ZL * b, ZL * b + 65), r("o16")], [("zt", 64 * b, 64 * b + 64)]
+            if b < 2:
+                act(o, i, F.Copy, rd, wr, scale=0.5)
+            else:
+                ts(o, i, 0.5, None, mult, None, rd, wr)
+        quant("zq%d" % t, "zs%d" % t, "zt", 0, 128)
+        send("z", t, to)
+        arrival("z", t, frm)
+        if t == 0:
+            fill("zero", 0, 512, 0.0)
+            fill("ht", 256, 512, 0.0)
+            ts(T.p16[:, 0:4], T.pi[:, 0:4], 16, None, AluOpType.bitwise_and, None, [r("pi")], [r("p16")])
+            for k in "zh":
+                quant(k + "c", k + "p", "zero", 0, 128)
+            ts(T.hi[:, 0:1], T.p16[:, 0:1], 0.0625, None, mult, None, [r("p16")], [r("hi")])
+            ts(T.lo[:, 0:1], T.p16[:, 0:1], -0.0625, 1.0, mult, add, [r("p16")], [r("lo")])
+        as_list("kr", "kw", 0.5, 31.5)
+        cp(T.cr[:, 16:272], T.rr[:, 0:64].indirect(T.kw[:, 0:16]), [r("rr"), r("kw")], [r("cr", 16, 272)])
+        if t < R - 1:
+            cp(T.ri[:, 0:64], T.rr[:, 0:64], [r("rr")], [r("ri")])
+            ts(T.rm[:, 0:64], T.ri[:, 0:64], 3, None, AluOpType.bitwise_and, None, [r("ri")], [r("rm")])
+            ts(T.rm4[:, 0:64], T.rm[:, 0:64], 4.0, None, mult, None, [r("rm")], [r("rm4")])
+        for b in range(4):
+            mm(b, "pw", 128, "wq", "wp", 128 * b, "zc", "zp", 64 + K * t)
+        for b in range(4):
+            o, i, rd, wr = T.ht[:, b:256:4], T.pw[:, 512 * b + 64:512 * b + 128], [bank("pw", b)], [("ht", 64 * b, 64 * b + 64)]
+            if b in (1, 3):
+                ts(o, i, 0.0, 0.03125, amax, mult, rd, wr)
+            else:
+                act(o, i, F.Relu, rd, wr, scale=0.03125)
+        quant("hq%d" % t, "hs%d" % t, "ht", 0, 128)
+        send("h", t, frm)
+        arrival("h", t, to)
+        if t < R - 1:
+            act(T.cm4[:, 0:256], T.rm4[:, 0:64].indirect(T.kw[:, 0:16]), F.Copy, [r("rm4"), r("kw")], [r("cm4")])
+        as_list("cr", "cw", 1.0, 0.0)
+        if t < R - 1:
+            prekeys_own()
+            prekeys_next()
+        else:
+            cp(T.cf[:, 0:256], T.cr[:, 16:272], [r("cr", 16, 272)], [r("cf")])
+            dma("y", "dol", T.ol[:], T.cf[0:128:16, 0:256], [r("cf")], [])
+            quant("qv", "sv", "vt", 0, 128)
+        new = "t%d" % (t + 1)
+        for b in range(4):
+            mm(b, "pw", 128, "eq", "esc", 128 * b, "hc", "hp", 64 + K * t)
+
+        def unpack(b):
+            o, i, rd, wr = T.dh[:, 64 * b:64 * b + 64], T.pw[:, 512 * b + 64:512 * b + 128], [bank("pw", b)], [r("dh", 64 * b, 64 * b + 64)]
+            if b == 0:
+                cp(o, i, rd, wr)
+            else:
+                act(o, i, F.Copy, rd, wr)
+
+        def gather(b, h):
+            o = C * (b - 2) + 128 * h
+            act(T.g2[:, o:o + 128], T.dh[:, 64 * b:64 * b + 64].indirect(T.cw[:, 8 * h:8 * h + 8]), F.Copy,
+                [r("dh", 64 * b, 64 * b + 64), r("cw")], [r("g2", o, o + 128)])
+        for b in range(4):
+            unpack(b)
+            if b > 1:
+                gather(b, 0)
+        gather(2, 1)
+        gather(3, 1)
+        for b in (0, 1):
+            tt(T[new][:, b:1024:4], T.dh[:, 64 * b:64 * b + 64].indirect(T.cw[:, 0:16]), T.fh[:, PL * b:PL * b + C], add,
+               [r("dh", 64 * b, 64 * b + 64), r("cw"), r("fh", PL * b, PL * b + C)], [(new, C * b, C * b + C)])
+        for h in range(2):
+            for b in (2, 3):
+                o, p, w = C * (b - 2) + 128 * h, 512 * b + 128 * h, C * b + 128 * h
+                tt(T[new][:, 512 * h + b:512 * h + 512:4], T.g2[:, o:o + 128], T.pf[:, p:p + 128], add,
+                   [r("g2", o, o + 128), bank("pf", b)], [(new, w, w + 128)])
+            quant("q%d" % (t + 1), "s%d" % (t + 1), new, 128 * h, 128, 128 * h)
+
+    def store_scales(qu, k):
+        dma(qu, "ds%d" % k, T.osc[4 * k:4 * k + 4, 0:256], T.s3[32 * k:32 * k + 4, 0:256], [r("s3")], [])
+    for h in range(2):
+        dma("y", "doc%d" % h, T.oc[:, 512 * h:512 * h + 512], T.q3[:, 128 * h:128 * h + 128].bitcast(dt.uint8), [r("q3", 128 * h, 128 * h + 128)], [])
+        mm(h, "pw", 128, "qv", "sv", 0, "q3", "s3", 128 * h)
+    act(T.yo[:, 0:128], T.pw[:, 0:128], F.Copy, [bank("pw", 0)], [r("yo", 0, 128)])
+    dma("s", "dy0", T.y[:, 0:128], T.yo[:, 0:128], [r("yo", 0, 128)], [])
+    cp(T.yo[:, 128:256], T.pw[:, 512:640], [bank("pw", 1)], [r("yo", 128, 256)])
+    store_scales("y", 0)
+    store_scales("y", 1)
+    store_scales("s", 2)
+    dma("s", "dy1", T.y[:, 128:256], T.yo[:, 128:256], [r("yo", 128, 256)], [])
+    store_scales("y", 3)
+    for sname in ("cv", "cs", "ct", "cg", "left"):
+        g.sync.wait_ge(T.sem[sname], count[sname])
+    for sname in DMAS:
+        if known["y"].get(sname, 0) < 16:
+            g.sync.wait_ge(T.sem[sname], 16)

@@ -2,26 +2,30 @@ from concourse.mybir import dt, AluOpType, AxisListType, ActivationFunctionType
 
 C, K, R = 256, 64, 3
 STEP = [1, 2, 4]
-PL = C + 16
-ZL = K + 16
+PL = C + 16 + K
 REV = (2, 3)
-HOR = 256
+HZ = 192
 CODES = "float8_e4m3fn_x4"
+WHOLE = 1.5 * 2.0 ** 23
+START = "hor0 hor1 strip p15 e0 kap e1 uoo e2 e3 kv ini coo cm4 pa nxo pb2 qu uu us half lasts cm16 x0 pk x1 d4"
+SEARCH = "g00 g01 k00 g10 g11 k01 k10 k11 p0 p1 m0 m1 s0 p2 t0 m2 s1 t1 p3 m3 s2 s3"
+MEANS = "f16 G r0 r1 r2 g0 g1 g2 g3 lt S red two X r16 s16 sc m0 O m1 o16 m2 m3 z0 z1"
 
 SCRATCH = {}
 for _n, _w, _d in (
-        ("ones", 512, "b"), ("strip", 516, "b"), ("zero", 512, "b"), ("eq", 512, "c"), ("esc", 512, "p"), ("ut", 512, "b"), ("qu", 128, "c"),
+        ("ones", 528, "b"), ("strip", 516, "b"), ("zero", 512, "b"), ("eq", 512, "c"), ("esc", 512, "p"), ("ut", 512, "b"), ("qu", 128, "c"),
         ("su", 128, "p"), ("uu", 256, "c"), ("us", 256, "p"), ("vt", 512, "b"), ("qv", 128, "c"), ("sv", 128, "p"), ("wq", 512, "c"), ("wp", 512, "p"),
-        ("nxi", 16, "i"), ("coi", 16, "i"), ("nxo", 16, "u"), ("coo", 16, "u"), ("uoi", 16, "i"), ("uoo", 16, "u"), ("iot", 272, "f"), ("pif", 1, "f"),
-        ("m4t", 64, "b"), ("pi", 4, "i"), ("p15", 4, "i"), ("p16", 4, "i"), ("si", 4, "i"), ("kap", 4, "f"), ("kv", 4, "f"),
-        ("lo", 1, "f"), ("hi", 1, "f"), ("nka", 1, "f"), ("fh", 4 * PL, "b"), ("sa", 256, "b"), ("sb", 256, "b"),
-        ("k1", 256, "b"), ("pk", 256, "b"), ("cm4", 256, "b"), ("cm16", 256, "b"), ("kr", 288, "b"), ("cr", 288, "b"), ("ta", 256, "b"),
-        ("tb", 288, "b"), ("e1", 32, "f"), ("kwf", 16, "f"), ("kw", 16, "u"), ("cw", 16, "u"), ("junk", 512, "b"), ("jun2", 256, "f"),
-        ("ww", 1024, "f"), ("acc", 4, "f"), ("fr", 64, "f"), ("lt", 65, "b"), ("f16", 4, "u"), ("s16", 4, "u"), ("r16", 4, "u"), ("o16", 4, "u"),
-        ("fi", 4, "i"), ("si2", 20, "i"), ("rr", 64, "b"), ("om", 256, "b"), ("ow", 256, "b"), ("g1", 256, "b"), ("zk", 4 * ZL, "b"),
-        ("zt", 512, "b"), ("ht", 512, "b"), ("ri", 64, "i"), ("rm", 64, "i"), ("rm4", 64, "b"), ("dh", 256, "b"), ("g2", 512, "b"), ("cf", 256, "f"),
+        ("nxi", 16, "i"), ("coi", 16, "i"), ("nxo", 16, "u"), ("coo", 16, "u"), ("uoi", 16, "i"), ("uoo", 16, "u"), ("iot", PL, "f"), ("pif", 1, "f"),
+        ("half", PL, "f"), ("m4t", 64, "b"), ("pi", 4, "i"), ("p15", 4, "i"), ("si", 4, "i"), ("kap", 4, "f"), ("kv", 4, "f"), ("ini", 4, "f"),
+        ("pa", 4, "i"), ("pb", 4, "f"), ("da", 16, "b"), ("d4", 64, "b"), ("d16", 256, "b"), ("s16t", 256, "b"),
+        ("fh", 4 * PL, "b"), ("sa", 256, "b"), ("sb", 256, "b"), ("hor", 8, "f"), ("sv8", 8, "f"), ("two", 8, "f"), ("sx8", 8, "f"),
+        ("k1", 256, "b"), ("pk", 256, "b"), ("cm4", 256, "b"), ("cm16", 256, "b"), ("kr", 256, "b"), ("cr", 256, "b"), ("pick", 256, "f"),
+        ("kw", 16, "u"), ("cw", 16, "u"), ("junk", 512, "b"), ("jun2", 256, "f"),
+        ("ww", 2048, "f"), ("acc", 4, "f"), ("lt", 65, "b"), ("f16", 4, "u"), ("g1", 256, "b"), ("s16", 4, "u"), ("r16", 4, "u"), ("o16", 16, "u"),
+        ("rr", 128, "b"), ("byr", 64, "b"), ("byo", 64, "f"), ("zk", 256, "b"),
+        ("zt", 512, "b"), ("ht", 512, "b"), ("dh", 256, "b"), ("g2", 512, "b"), ("cf", 256, "f"),
         ("yo", 256, "f"), ("w0", 256, "b"), ("w1", 256, "b"),
-        ("zc", 128 + R * K, "c"), ("zp", 128 + R * K, "p"), ("hc", 128 + R * K, "c"), ("hp", 128 + R * K, "p")):
+        ("zc", 128 + R * K, "c"), ("zp", 128 + R * K, "p"), ("hc", 128 + R * HZ, "c"), ("hp", 128 + R * HZ, "p")):
     SCRATCH[_n] = ("sbuf", [128, _w], {"b": "bfloat16", "c": CODES, "p": "uint8", "i": "int32", "u": "uint16", "f": "float32"}[_d])
 for _n in ("pf", "pw"):
     SCRATCH[_n] = ("psum", [128, 2048], "float32")
@@ -83,8 +87,8 @@ def rank_program(g, core, T, topo):
             book.append((reg[1], reg[2], q, s, n))
             read[reg[0]] = book
 
-    def op(q, call, reads, writes):
-        need(q, reads, writes)
+    def op(q, call, reads, writes, behind=False):
+        need(q, reads, [] if behind else writes)
         s = "c" + q
         count[s] += 1
         call().then_inc(T.sem[s], 1)
@@ -110,8 +114,8 @@ def rank_program(g, core, T, topo):
         op("v", lambda: V.quantize_mx(T[qb][:, a:a + n], T[sb_][:, a:a + n], T[tile][:, 4 * c0:4 * (c0 + n)]),
            src, [r(qb, a, a + n), r(sb_, a, a + n)])
 
-    def fill(name, a, b, val):
-        op("v", lambda: V.memset(T[name][:, a:b], val), [], [r(name, a, b)])
+    def fill(name, a, b, val, step=1):
+        op("v", lambda: V.memset(T[name][:, a:b:step], val), [], [r(name, a, b)])
 
     def whole(name, a, b, pattern, base=0, per=0):
         op("g", lambda: g.iota(T[name][:, a:b], pattern, base, per, allow_small_or_imprecise_dtypes=True), [], [r(name, a, b)])
@@ -128,16 +132,28 @@ def rank_program(g, core, T, topo):
     def cp(out, a, reads, writes):
         op("v", lambda: V.tensor_copy(out, a), reads, writes)
 
+    def horner(out, d0, d1, first, reads, writes):
+        op("v", lambda: V.tensor_tensor_scan(out, d0, d1, first, mult, add), reads, writes)
+
     def act(out, a, f, reads, writes, **kw):
         op("s", lambda: S.activation(out, a, f, **kw), reads, writes)
 
-    def mm(bank, buf, n, lq, ls, la, rq, rs, ra):
-        op("t", lambda: PE.matmul_mx(T[buf][:, 512 * bank:512 * bank + n], T[lq][:, la:la + 128], T[ls][:, la:la + 128],
-                                     T[rq][:, ra:ra + n], T[rs][:, ra:ra + n], True, True),
-           [r(lq, la, la + 128), r(ls, la, la + 128), r(rq, ra, ra + n), r(rs, ra, ra + n)], [(buf, 512 * bank, 512 * bank + 512)])
+    def copy(on, out, a, reads, writes):
+        if on == "s":
+            act(out, a, F.Copy, reads, writes)
+        else:
+            cp(out, a, reads, writes)
 
     def bank(buf, b):
         return (buf, 512 * b, 512 * b + 512)
+
+    def mm(b, buf, n, lq, ls, la, rq, rs, ra, start=True, stop=True):
+        op("t", lambda: PE.matmul_mx(T[buf][:, 512 * b:512 * b + n], T[lq][:, la:la + 128], T[ls][:, la:la + 128],
+                                     T[rq][:, ra:ra + n], T[rs][:, ra:ra + n], start, stop),
+           [r(lq, la, la + 128), r(ls, la, la + 128), r(rq, ra, ra + n), r(rs, ra, ra + n)], [bank(buf, b)], not start)
+
+    def landing(kind, t):
+        return 128 + (K if kind == "z" else HZ) * t
 
     def send(kind, t, peer):
         cq, sq = kind + "q%d" % t, kind + "s%d" % t
@@ -145,28 +161,30 @@ def rank_program(g, core, T, topo):
         dst = T.cores[peer]
         rid, pid, _se = topo.addr(dst)
         m, arr = topo.mask(core, dst), T.sem[kind + "a%d" % t]
-        a, e = 128 + K * t, 128 + K * t + K
-        g.remote_dma(T[kind + "c"][:, a:e].bitcast(dt.uint8), T[cq][:, 0:64].bitcast(dt.uint8), arr, T.sem.left, pid, rid, m)
-        g.remote_dma(T[kind + "p"][:, a:e], T[sq][:, 0:64], arr, T.sem.left, pid, rid, m)
+        a = landing(kind, t)
+        g.remote_dma(T[kind + "c"][:, a:a + K].bitcast(dt.uint8), T[cq][:, 0:64].bitcast(dt.uint8), arr, T.sem.left, pid, rid, m)
+        g.remote_dma(T[kind + "p"][:, a:a + K], T[sq][:, 0:64], arr, T.sem.left, pid, rid, m)
         count["left"] += 2 * len(topo.engines(core, dst))
 
     def arrival(kind, t, peer):
         n = 2 * len(topo.engines(T.cores[peer], core))
-        a, e = 128 + K * t, 128 + K * t + K
-        note("r", [], [(kind + "c", a, e), (kind + "p", a, e)], kind + "a%d" % t, n)
+        a = landing(kind, t)
+        note("r", [], [(kind + "c", a, a + K), (kind + "p", a, a + K)], kind + "a%d" % t, n)
 
-    def as_list(row, dest, scale, base):
-        op("v", lambda: V.transpose(T.ta[:, 0:256], T[row][:, 16:272]), [r(row)], [r("ta")])
-        op("v", lambda: V.transpose(T.tb[:, 0:288], T[row][:, 0:288]), [r(row)], [r("tb")])
-        for k, (src, a, m) in enumerate((("ta", 0, "lo"), ("ta", 16, "hi"), ("tb", 16, "hi"), ("tb", 32, "lo"))):
-            end = 288 if a == 32 else 256
-            ts(T.e1[:, 8 * k:8 * k + 8], T[src][:, a:end:32], T[m][:, 0:1], None, mult, None, [r(src), r(m)], [r("e1", 8 * k, 8 * k + 8)])
-        tt(T.kwf[:, 0:16:2], T.e1[:, 0:8], T.e1[:, 16:24], add, [r("e1", 0, 8), r("e1", 16, 24)], [("kwf", 0, 8)])
-        tt(T.kwf[:, 1:16:2], T.e1[:, 8:16], T.e1[:, 24:32], add, [r("e1", 8, 16), r("e1", 24, 32)], [("kwf", 8, 16)])
-        ts(T[dest][:, 0:16], T.kwf[:, 0:16], scale, base, mult, add, [r("kwf")], [r(dest)])
+    def picker(name, slots, n, run, col):
+        q = T.kap[:, 0:1]
+        ts(T[name][:, 0:n], T[slots][:, 0:n], q, 256.0, AluOpType.is_gt, mult, [r(slots), r("kap")], [r(name)])
+        ts(T.da[:, 0:run], T[slots][:, 0:run], q, 2.0 ** -8, AluOpType.is_le, amax, [r(slots), r("kap")], [r("da")])
+        op("v", lambda: V.tensor_reduce(T.pb[:, col:col + 1], T.da[:, 0:run], AxisListType.X, mult), [r("da")], [r("pb", col, col + 1)])
+
+    def as_list(row, dest, base):
+        horner(T.pick[:, 0:256], T.d16[:, 0:256], T[row][:, 0:256], 0.0, [r("d16"), r(row)], [r("pick")])
+        ts(T[dest][:, 0:16], T.pick[:, 15:256:16], T.pb[:, 1:2], base, mult, add, [r("pick"), r("pb", 1, 2)], [r(dest)])
 
     def prekeys_own():
-        act(T.cm16[:, 0:256], T.cm4[:, 0:256], F.Copy, [r("cm4")], [r("cm16")], bias=2.0, scale=4.0)
+        for h in range(2):
+            a, e = 128 * h, 128 * h + 128
+            ts(T.cm16[:, a:e], T.cm4[:, a:e], 4.0, 2.0 - h, mult, add, [r("cm4")], [r("cm16", a, e)])
 
     def prekeys_next():
         tt(T.pk[:, 0:256], T.cm4[:, 0:256].indirect(T.nxo[:, 0:16]), T.cm16[:, 0:256], add, [r("cm4"), r("nxo"), r("cm16")], [r("pk")])
@@ -179,44 +197,64 @@ def rank_program(g, core, T, topo):
     fill("strip", 0, 516, 0.0)
     whole("pif", 0, 1, [[0, 1]], 0, 1)
     whole("iot", 0, 128, [[1, 128]])
-    whole("m4t", 0, 64, [[0, 16], [4, 4]])
-    whole("uoi", 0, 16, [[1, 2], [16, 8]])
     whole("pi", 0, 4, [[0, 4]], 0, 1)
     whole("si", 0, 4, [[16, 4]])
-    whole("ones", 0, 512, [[0, 512]], 1)
-    whole("iot", 128, 272, [[1, 144]], 128)
-    ts(T.strip[:, 3:515:4], T.iot[:, 0:128], T.pif[:, 0:1], None, AluOpType.is_equal, None, [r("iot", 0, 128), r("pif")], [r("strip", 3, 515)])
-    cp(T.uoo[:, 0:16], T.uoi[:, 0:16], [r("uoi")], [r("uoo")])
-    cp(T.coo[:, 0:16], T.coi[:, 0:16], [r("coi")], [r("coo")])
-    for b in range(4):
+    whole("m4t", 0, 64, [[0, 16], [4, 4]])
+    whole("uoi", 0, 16, [[1, 2], [16, 8]])
+    whole("iot", 128, PL, [[1, PL - 128]], 128)
+    whole("ones", 16, 528, [[0, 512]], 1)
+
+    def const(b):
         op("v", lambda: V.quantize_mx(T.eq[:, 128 * b:128 * b + 128], T.esc[:, 128 * b:128 * b + 128], T.strip[:, 3 - b:515 - b]),
            [r("strip")], [r("eq", 128 * b, 128 * b + 128), r("esc", 128 * b, 128 * b + 128)])
-    ts(T.p15[:, 0:4], T.pi[:, 0:4], 15, None, AluOpType.bitwise_and, None, [r("pi")], [r("p15")])
-    act(T.cm4[:, 0:256], T.m4t[:, 0:64].indirect(T.coo[:, 0:16]), F.Copy, [r("m4t"), r("coo")], [r("cm4")])
-    tt(T.kap[:, 0:4], T.p15[:, 0:4], T.si[:, 0:4], add, [r("p15"), r("si")], [r("kap")])
-    cp(T.nxo[:, 0:16], T.nxi[:, 0:16], [r("nxi")], [r("nxo")])
-    quant("qu", "su", "ut", 0, 128)
-    cp(T.uu[:, 0:256].bitcast(dt.uint32), T.qu[:, 0:128].bitcast(dt.uint32).indirect(T.uoo[:, 0:16]), [r("qu"), r("uoo")], [r("uu")])
-    prekeys_own()
-    act(T.us[:, 0:256], T.su[:, 0:128].indirect(T.uoo[:, 0:16]), F.Copy, [r("su"), r("uoo")], [r("us")])
+
+    def lasts():
+        for i in range(2):
+            act(T.ones[:, 271 + 256 * i:272 + 256 * i], T.ini[:, i:i + 1], F.Copy, [r("ini")], [r("ones", 271 + 256 * i, 272 + 256 * i)])
+    steps = {
+        "hor0": lambda: fill("hor", 0, 8, 0.0, 2),
+        "hor1": lambda: fill("hor", 1, 8, -1023.0 / 1024.0, 2),
+        "strip": lambda: ts(T.strip[:, 3:515:4], T.iot[:, 0:128], T.pif[:, 0:1], None, AluOpType.is_equal, None,
+                            [r("iot", 0, 128), r("pif")], [r("strip", 3, 515)]),
+        "p15": lambda: ts(T.p15[:, 0:4], T.pi[:, 0:4], 15, None, AluOpType.bitwise_and, None, [r("pi")], [r("p15")]),
+        "kap": lambda: tt(T.kap[:, 0:4], T.p15[:, 0:4], T.si[:, 0:4], add, [r("p15"), r("si")], [r("kap")]),
+        "pa": lambda: ts(T.pa[:, 0:1], T.pi[:, 0:1], 3, None, AluOpType.bitwise_and, None, [r("pi")], [r("pa")]),
+        "uoo": lambda: cp(T.uoo[:, 0:16], T.uoi[:, 0:16], [r("uoi")], [r("uoo")]),
+        "pb2": lambda: ts(T.pb[:, 2:3], T.pa[:, 0:1], 64.0, 0.125, mult, add, [r("pa")], [r("pb", 2, 3)]),
+        "d4": lambda: picker("d4", "m4t", 64, 4, 0),
+        "kv": lambda: act(T.kv[:, 0:4], T.kap[:, 0:4], F.Copy, [r("kap")], [r("kv")], bias=-63.0, scale=2.0),
+        "ini": lambda: act(T.ini[:, 0:4], T.kap[:, 0:4], F.Copy, [r("kap")], [r("ini")], bias=17.0),
+        "half": lambda: act(T.half[:, 0:PL], T.iot[:, 0:PL], F.Copy, [r("iot")], [r("half")], bias=0.5),
+        "coo": lambda: cp(T.coo[:, 0:16], T.coi[:, 0:16], [r("coi")], [r("coo")]),
+        "qu": lambda: quant("qu", "su", "ut", 0, 128),
+        "cm4": lambda: act(T.cm4[:, 0:256], T.m4t[:, 0:64].indirect(T.coo[:, 0:16]), F.Copy, [r("m4t"), r("coo")], [r("cm4")]),
+        "uu": lambda: cp(T.uu[:, 0:256].bitcast(dt.uint32), T.qu[:, 0:128].bitcast(dt.uint32).indirect(T.uoo[:, 0:16]),
+                         [r("qu"), r("uoo")], [r("uu")]),
+        "us": lambda: act(T.us[:, 0:256], T.su[:, 0:128].indirect(T.uoo[:, 0:16]), F.Copy, [r("su"), r("uoo")], [r("us")]),
+        "cm16": prekeys_own,
+        "lasts": lasts,
+        "x0": lambda: quant("q0", "s0", "t0", 0, 128, 0),
+        "x1": lambda: quant("q0", "s0", "t0", 128, 128, 128),
+        "nxo": lambda: cp(T.nxo[:, 0:16], T.nxi[:, 0:16], [r("nxi")], [r("nxo")]),
+        "pk": prekeys_next,
+    }
+    for b in range(4):
+        steps["e%d" % b] = lambda b=b: const(b)
+    for w in START.split():
+        steps[w]()
     need("y", [r("t0")], [])
     dma("y", "dwc", T.wq[:, 0:512].bitcast(dt.uint8), T.wc[:, 0:2048], [], [r("wq")])
     dma("y", "dws", T.wp[:, 0:512], T.ws[:, 0:512], [], [r("wp")])
     dma("y", "dv", T.vt[:], T.v[:], [], [r("vt")])
-    quant("q0", "s0", "t0", 0, 128, 0)
-    prekeys_next()
-    ts(T.kv[:, 0:4], T.kap[:, 0:4], 2.0, -63.0, mult, add, [r("kap")], [r("kv")])
-    ts(T.nka[:, 0:1], T.kap[:, 3:4], -256.0, None, mult, None, [r("kap")], [r("nka")])
-    quant("q0", "s0", "t0", 128, 128, 128)
-    whole("ones", HOR, HOR + 1, [[0, 1]])
+    whole("ones", 15, 16, [[0, 1]])
     whole("lt", 64, 65, [[0, 1]], -64)
     for b in range(4):
-        whole("fh", PL * b + C, PL * b + PL, [[0, 16]])
-        whole("zk", ZL * b, ZL * b + 1, [[0, 1]])
+        whole("fh", PL * b + C, PL * b + PL, [[0, PL - C]])
+    whole("two", 0, 8, [[0, 8]])
     whole("zt", 256, 512, [[0, 256]])
-    for n in ("kr", "cr"):
-        whole(n, 0, 16, [[0, 16]])
-        whole(n, 272, 288, [[0, 16]])
+    whole("byr", 0, 64, [[0, 64]])
+    whole("s16t", 0, 256, [[0, 16], [1, 16]])
+    whole("rr", 0, 128, [[0, 128]])
 
     for t in range(R):
         q, s = "q%d" % t, "s%d" % t
@@ -226,111 +264,106 @@ def rank_program(g, core, T, topo):
                 mm(2 * h + k, "pw", 128, "uu", "us", 128 * k, q, s, 128 * h)
         for b in range(4):
             mm(b, "pf", 256, "eq", "esc", 128 * b, q, s, 0)
-        for h, k in ((0, 0), (0, 1), (1, 0), (1, 1)):
-            n, a, e = ("sa", "sb")[k], 128 * h, 128 * h + 128
-            act(T[n][:, a:e], T.pw[:, 1024 * h + 512 * k:1024 * h + 512 * k + 128], F.Sign, [bank("pw", 2 * h + k)], [r(n, a, e)],
-                bias=-1e-36, scale=-1.0)
-        for a, e in ((0, 128), (128, 256)):
-            tt(T.k1[:, a:e], T.sa[:, a:e], T.pk[:, a:e], add, [r("sa", a, e), r("pk", a, e)], [r("k1", a, e)])
-            tt(T.kr[:, 16 + a:16 + e], T.k1[:, a:e], T.sb[:, a:e], mult, [r("k1", a, e), r("sb", a, e)], [r("kr", 16 + a, 16 + e)])
 
-        def plane_f(b):
+        def sign(h, k):
+            n, a, e = ("sa", "sb")[k], 128 * h, 128 * h + 128
+            i = T.pw[:, 1024 * h + 512 * k:1024 * h + 512 * k + 128]
+            if (h, k) == (1, 0):
+                ts(T[n][:, a:e], i, 0.0, 2.0, AluOpType.is_lt, mult, [bank("pw", 2 * h + k)], [r(n, a, e)])
+            else:
+                act(T[n][:, a:e], i, F.Sign, [bank("pw", 2 * h + k)], [r(n, a, e)], bias=-1e-36, scale=-1.0)
+
+        def key(h, k):
+            a, e = 128 * h, 128 * h + 128
+            if k == 0:
+                tt(T.k1[:, a:e], T.sa[:, a:e], T.pk[:, a:e], add, [r("sa", a, e), r("pk", a, e)], [r("k1", a, e)])
+            else:
+                tt(T.kr[:, a:e], T.k1[:, a:e], T.sb[:, a:e], mult, [r("k1", a, e), r("sb", a, e)], [r("kr", a, e)])
+
+        def plane(b):
             act(T.fh[:, PL * b:PL * b + C], T.pf[:, 512 * b:512 * b + C], F.Copy, [bank("pf", b)], [r("fh", PL * b, PL * b + C)])
 
         def mask(i):
-            ts(T["m%d" % i][:, 0:256], T.kr[:, 16:272], T.kv[:, i:i + 1], 2.0 ** -10, AluOpType.not_equal, amax,
-               [r("kr", 16, 272), r("kv")], [r("m%d" % i, 0, 256)])
+            ts(T["m%d" % i][:, 0:256], T.kr[:, 0:256], T.kv[:, i:i + 1], 2.0 ** -10, AluOpType.not_equal, amax,
+               [r("kr"), r("kv")], [r("m%d" % i, 0, 256)])
 
         def scan(i):
+            a = 512 * i + 256
             if i in REV:
-                op("v", lambda: V.tensor_tensor_scan(T.ww[:, 256 * i + 255:256 * i - 1:-1], T["m%d" % i][:, 255::-1],
-                                                     T.ones[:, HOR + 255:HOR - 1:-1], 1.0, mult, add),
-                   [r("m%d" % i), r("ones", HOR, HOR + 256)], [r("ww", 256 * i, 256 * i + 256)])
+                horner(T.ww[:, a + 255:a - 1:-1], T["m%d" % i][:, 255::-1], T.ones[:, 270:14:-1], T.ini[:, i:i + 1],
+                       [r("m%d" % i), r("ones", 15, 271), r("ini")], [r("ww", a, a + 256)])
             else:
-                op("v", lambda: V.tensor_tensor_scan(T["w%d" % i][:, 0:256], T["m%d" % i][:, 0:256], T.ones[:, 0:256], 1.0, mult, mult),
-                   [r("m%d" % i), r("ones", 0, 256)], [r("w%d" % i)])
+                op("v", lambda: V.tensor_tensor_scan(T["w%d" % i][:, 0:256], T["m%d" % i][:, 0:256], T.ones[:, 16 + 256 * i:272 + 256 * i],
+                                                     1.0, mult, mult),
+                   [r("m%d" % i), r("ones", 16 + 256 * i, 272 + 256 * i)], [r("w%d" % i)])
 
         def total(i):
+            a = 512 * i + 256
             act(T.junk[:, 256 * i:256 * i + 256], T["w%d" % i][:, 0:256], F.Copy, [r("w%d" % i)],
-                [r("junk", 256 * i, 256 * i + 256), r("ww", 256 * i, 256 * i + 1)], accum_out=T.ww[:, 256 * i:256 * i + 1])
-        plane_f(0)
-        plane_f(1)
-        mask(0)
-        mask(1)
-        scan(0)
-        plane_f(2)
-        total(0)
-        mask(2)
-        scan(1)
-        total(1)
-        plane_f(3)
-        mask(3)
-        scan(2)
-        scan(3)
-        vv, rv = T.ww[:, 0:1024:256], [r("ww", 256 * i, 256 * i + 1) for i in range(4)]
-        d = [T.si2[:, 4 * k:4 * k + 4] for k in range(5)]
-        e = [r("si2", 4 * k, 4 * k + 4) for k in range(5)]
-        cp(T.f16[:, 0:4], vv, rv, [r("f16")])
-        ts(d[0], vv, 1024.0, None, mult, None, rv, [e[0]])
-        ts(T.fr[:, 0:64], T.iot[:, 0:272].indirect(T.f16[:, 0:4]), 1.0 - 2.0 ** -10, None, mult, None, [r("iot"), r("f16")], [r("fr")])
-        for i in range(3):
-            act(T.jun2[:, 64 * i:64 * i + 64], T.fr[:, 0:64], F.Sign, [r("fr"), rv[i]], [r("jun2", 64 * i, 64 * i + 64), r("acc", i, i + 1)],
-                bias=T.ww[:, 256 * i:256 * i + 1], scale=-1.0, accum_out=T.acc[:, i:i + 1])
-        for b in range(4):
-            act(T.g1[:, 64 * b:64 * b + 64], T.fh[:, PL * b:PL * b + PL].indirect(T.f16[:, 0:4]), F.Copy,
-                [r("fh", PL * b, PL * b + PL), r("f16")], [r("g1", 64 * b, 64 * b + 64)])
+                [r("junk", 256 * i, 256 * i + 256), r("ww", a, a + 1)], accum_out=T.ww[:, a:a + 1])
+        steps = {"g": sign, "k": key, "p": plane, "m": mask, "s": scan, "t": total}
+        for w in SEARCH.split():
+            steps[w[0]](*[int(ch) for ch in w[1:]])
+
+        vv, rv = T.ww[:, 256:2048:512], [r("ww", 512 * i + 256, 512 * i + 257) for i in range(4)]
+        rg = [r("ww", 512 * i, 512 * i + 1) for i in range(4)]
+        row, rrow = T.half[:, 0:PL].indirect(T.f16[:, 0:4]), [r("half"), r("f16")]
+
+        def rank_of_key(i):
+            act(T.jun2[:, 64 * i:64 * i + 64], row, F.Sign, rrow + [rv[i]], [r("jun2", 64 * i, 64 * i + 64), r("acc", i, i + 1)],
+                bias=T.ww[:, 512 * i + 256:512 * i + 257], scale=-1.0, accum_out=T.acc[:, i:i + 1])
+
+        def first(b, on):
+            copy(on, T.g1[:, 64 * b:64 * b + 64], T.fh[:, PL * b:PL * b + PL].indirect(T.f16[:, 0:4]),
+                 [r("fh", PL * b, PL * b + PL), r("f16")], [r("g1", 64 * b, 64 * b + 64)])
 
         def mean(b):
-            tt(T.zk[:, ZL * b + 1:ZL * b + 65], T.fh[:, PL * b:PL * b + PL].indirect(T.s16[:, 0:4]), T.g1[:, 64 * b:64 * b + 64], add,
-               [r("fh", PL * b, PL * b + PL), r("s16"), r("g1", 64 * b, 64 * b + 64)], [r("zk", ZL * b + 1, ZL * b + 65)])
-        ts(T.fi[:, 0:4], d[0], 10, None, AluOpType.arith_shift_right, None, [e[0]], [r("fi")])
-        ts(d[1], d[0], 1023, None, AluOpType.bitwise_and, None, [e[0]], [e[1]])
-        ts(T.lt[:, 0:64], T.fr[:, 0:64], T.ww[:, 768:769], 2.0, AluOpType.is_lt, mult, [r("fr"), rv[3]], [r("lt", 0, 64)])
-        tt(d[2], T.fi[:, 0:4], d[1], add, [r("fi"), e[1]], [e[2]])
-        op("v", lambda: V.tensor_reduce(T.acc[:, 3:4], T.lt[:, 0:65], AxisListType.X, add), [r("lt")], [r("acc", 3, 4)])
-        ts(d[3], d[2], 255, None, AluOpType.bitwise_and, None, [e[2]], [e[3]])
-        tt(d[4], d[3], T.fi[:, 0:4], amax, [e[3], r("fi")], [e[4]])
-        ts(T.r16[:, 0:4], T.acc[:, 0:4], 0.5, 31.0, mult, add, [r("acc")], [r("r16")])
-        cp(T.s16[:, 0:4], d[4], [e[4]], [r("s16")])
-        cp(T.rr[:, 0:64], T.iot[:, 0:272].indirect(T.r16[:, 0:4]), [r("iot"), r("r16")], [r("rr")])
-        mean(0)
-        for i in range(4):
-            if i < 3:
-                ts(T.om[:, 64 * i:64 * i + 64], T.rr[:, 0:64], T.kap[:, i:i + 1], 256.0, AluOpType.not_equal, mult,
-                   [r("rr"), r("kap")], [r("om", 64 * i, 64 * i + 64)])
-            else:
-                act(T.om[:, 64 * i:64 * i + 64], T.rr[:, 0:64], F.Abs, [r("rr"), r("nka")], [r("om", 64 * i, 64 * i + 64)],
-                    bias=T.nka[:, 0:1], scale=256.0)
-        mean(1)
-        op("v", lambda: V.tensor_tensor_scan(T.ow[:, 0:256], T.ones[:, 0:256], T.om[:, 0:256], 0.0, add, AluOpType.min),
-           [r("ones", 0, 256), r("om")], [r("ow")])
-        mean(2)
-        ts(T.o16[:, 0:4], T.ow[:, 63:256:64], -1.0, 64.0, mult, add, [r("ow")], [r("o16")])
-        mean(3)
-        for b in range(4):
-            o, i, rd, wr = T.zt[:, b:256:4], T.zk[:, ZL * b:ZL * b + 65].indirect(T.o16[:, 0:4]), \
-                [r("zk", ZL * b, ZL * b + 65), r("o16")], [("zt", 64 * b, 64 * b + 64)]
-            if b < 2:
+            tt(T.zk[:, 64 * b:64 * b + 64], T.fh[:, PL * b:PL * b + PL].indirect(T.s16[:, 0:4]), T.g1[:, 64 * b:64 * b + 64], add,
+               [r("fh", PL * b, PL * b + PL), r("s16"), r("g1", 64 * b, 64 * b + 64)], [r("zk", 64 * b, 64 * b + 64)])
+
+        def final(h):
+            o, i, rd, wr = T.zt[:, 128 * h:128 * h + 128], T.zk[:, 0:256].indirect(T.o16[:, 8 * h:8 * h + 8]), \
+                [r("zk"), r("o16")], [("zt", 128 * h, 128 * h + 128)]
+            if h == 0:
                 act(o, i, F.Copy, rd, wr, scale=0.5)
             else:
                 ts(o, i, 0.5, None, mult, None, rd, wr)
+        steps = {
+            "f16": lambda: cp(T.f16[:, 0:4], vv, rv, [r("f16")]),
+            "two": lambda: ts(T.two[:, 0:8:2], T.sv8[:, 1:8:2], 0.25, 1024.0, AluOpType.is_lt, mult, [r("sv8")], [r("two")]),
+            "X": lambda: op("v", lambda: V.tensor_tensor_scan(T.sx8[:, 7::-1], T.two[:, 7::-1], T.sv8[:, 7::-1], 0.0, mult, amax),
+                            [r("two"), r("sv8")], [r("sx8")]),
+            "G": lambda: ts(T.ww[:, 0:2048:512], vv, WHOLE, -WHOLE, add, add, rv, rg),
+            "S": lambda: horner(T.sv8[:, 0:8], T.hor[:, 0:8], T.ww[:, 0:2048:256], 0.0, [r("hor")] + rv + rg, [r("sv8")]),
+            "s16": lambda: ts(T.s16[:, 0:4], T.sx8[:, 0:8:2], 0.0625, None, add, None, [r("sx8")], [r("s16")]),
+            "lt": lambda: ts(T.lt[:, 0:64], row, T.ww[:, 1792:1793], 2.0, AluOpType.is_lt, mult, rrow + [rv[3]], [r("lt", 0, 64)]),
+            "red": lambda: op("v", lambda: V.tensor_reduce(T.acc[:, 3:4], T.lt[:, 0:65], AxisListType.X, add), [r("lt")], [r("acc", 3, 4)]),
+            "r16": lambda: ts(T.r16[:, 0:4], T.acc[:, 0:4], 0.5, 32.0, mult, add, [r("acc")], [r("r16")]),
+            "sc": lambda: cp(T.byr[:, 0:64].indirect(T.r16[:, 0:4]), T.iot[:, 0:64], [r("iot"), r("r16")], [r("byr")]),
+            "O": lambda: horner(T.byo[:, 0:64], T.d4[:, 0:64], T.byr[:, 0:64], 0.0, [r("d4"), r("byr")], [r("byo")]),
+            "o16": lambda: ts(T.o16[:, 0:16], T.byo[:, 3:64:4], T.pb[:, 0:1], T.pb[:, 2:3], mult, add, [r("byo"), r("pb", 0, 3)], [r("o16")]),
+        }
+        for i in range(4):
+            steps["r%d" % i] = lambda i=i: rank_of_key(i)
+            steps["g%d" % i] = lambda i=i: first(i, "s")
+            steps["v%d" % i] = lambda i=i: first(i, "v")
+            steps["m%d" % i] = lambda i=i: mean(i)
+            steps["z%d" % i] = lambda i=i: final(i)
+        for w in MEANS.split():
+            steps[w]()
         quant("zq%d" % t, "zs%d" % t, "zt", 0, 128)
         send("z", t, to)
         arrival("z", t, frm)
         if t == 0:
             fill("zero", 0, 512, 0.0)
+            picker("d16", "s16t", 256, 16, 1)
+            quant("zc", "zp", "zero", 0, 128)
             fill("ht", 256, 512, 0.0)
-            ts(T.p16[:, 0:4], T.pi[:, 0:4], 16, None, AluOpType.bitwise_and, None, [r("pi")], [r("p16")])
-            for k in "zh":
-                quant(k + "c", k + "p", "zero", 0, 128)
-            ts(T.hi[:, 0:1], T.p16[:, 0:1], 0.0625, None, mult, None, [r("p16")], [r("hi")])
-            ts(T.lo[:, 0:1], T.p16[:, 0:1], -0.0625, 1.0, mult, add, [r("p16")], [r("lo")])
-        as_list("kr", "kw", 0.5, 31.5)
-        cp(T.cr[:, 16:272], T.rr[:, 0:64].indirect(T.kw[:, 0:16]), [r("rr"), r("kw")], [r("cr", 16, 272)])
-        if t < R - 1:
-            cp(T.ri[:, 0:64], T.rr[:, 0:64], [r("rr")], [r("ri")])
-            ts(T.rm[:, 0:64], T.ri[:, 0:64], 3, None, AluOpType.bitwise_and, None, [r("ri")], [r("rm")])
-            ts(T.rm4[:, 0:64], T.rm[:, 0:64], 4.0, None, mult, None, [r("rm")], [r("rm4")])
+        ts(T.rr[:, 0:128:2], T.half[:, 0:64].indirect(T.r16[:, 0:4]), -0.5, None, add, None, [r("half"), r("r16")], [r("rr")])
+        as_list("kr", "kw", 63.25)
+        crow = "cr" if t < R - 1 else "cf"
+        cp(T[crow][:, 0:256], T.rr[:, 0:128].indirect(T.kw[:, 0:16]), [r("rr"), r("kw")], [r(crow)])
+        as_list(crow, "cw", 0.125)
         for b in range(4):
             mm(b, "pw", 128, "wq", "wp", 128 * b, "zc", "zp", 64 + K * t)
         for b in range(4):
@@ -342,37 +375,26 @@ def rank_program(g, core, T, topo):
         quant("hq%d" % t, "hs%d" % t, "ht", 0, 128)
         send("h", t, frm)
         arrival("h", t, to)
+        if t == 0:
+            for k in range(R + 1):
+                quant("hc", "hp", "zero", HZ * k, 128)
         if t < R - 1:
-            act(T.cm4[:, 0:256], T.rm4[:, 0:64].indirect(T.kw[:, 0:16]), F.Copy, [r("rm4"), r("kw")], [r("cm4")])
-        as_list("cr", "cw", 1.0, 0.0)
-        if t < R - 1:
+            cp(T.cm4[:, 0:256], T.m4t[:, 0:64].indirect(T.cw[:, 0:16]), [r("m4t"), r("cw")], [r("cm4")])
             prekeys_own()
             prekeys_next()
         else:
-            cp(T.cf[:, 0:256], T.cr[:, 16:272], [r("cr", 16, 272)], [r("cf")])
             dma("y", "dol", T.ol[:], T.cf[0:128:16, 0:256], [r("cf")], [])
             quant("qv", "sv", "vt", 0, 128)
         new = "t%d" % (t + 1)
         for b in range(4):
-            mm(b, "pw", 128, "eq", "esc", 128 * b, "hc", "hp", 64 + K * t)
-
-        def unpack(b):
-            o, i, rd, wr = T.dh[:, 64 * b:64 * b + 64], T.pw[:, 512 * b + 64:512 * b + 128], [bank("pw", b)], [r("dh", 64 * b, 64 * b + 64)]
-            if b == 0:
-                cp(o, i, rd, wr)
-            else:
-                act(o, i, F.Copy, rd, wr)
-
-        def gather(b, h):
-            o = C * (b - 2) + 128 * h
-            act(T.g2[:, o:o + 128], T.dh[:, 64 * b:64 * b + 64].indirect(T.cw[:, 8 * h:8 * h + 8]), F.Copy,
-                [r("dh", 64 * b, 64 * b + 64), r("cw")], [r("g2", o, o + 128)])
-        for b in range(4):
-            unpack(b)
-            if b > 1:
-                gather(b, 0)
-        gather(2, 1)
-        gather(3, 1)
+            mm(min(b, 2), "pw", 128, "eq", "esc", 128 * b, "hc", "hp", landing("h", t) - 64 * (b == 3), b != 3, b != 2)
+        for b, n, on in ((0, 64, "v"), (1, 64, "s"), (2, 128, "s")):
+            copy(on, T.dh[:, 64 * b:64 * b + n], T.pw[:, 512 * b:512 * b + n], [bank("pw", b)], [r("dh", 64 * b, 64 * b + n)])
+        for h in range(2):
+            for b in (2, 3):
+                o = C * (b - 2) + 128 * h
+                act(T.g2[:, o:o + 128], T.dh[:, 64 * b:64 * b + 64].indirect(T.cw[:, 8 * h:8 * h + 8]), F.Copy,
+                    [r("dh", 64 * b, 64 * b + 64), r("cw")], [r("g2", o, o + 128)])
         for b in (0, 1):
             tt(T[new][:, b:1024:4], T.dh[:, 64 * b:64 * b + 64].indirect(T.cw[:, 0:16]), T.fh[:, PL * b:PL * b + C], add,
                [r("dh", 64 * b, 64 * b + 64), r("cw"), r("fh", PL * b, PL * b + C)], [(new, C * b, C * b + C)])

@@ -3,29 +3,33 @@ from concourse.mybir import dt, AluOpType, AxisListType, ActivationFunctionType
 C, K, R = 256, 64, 3
 STEP = [1, 2, 4]
 PL = C + 16 + K
-REV = (2, 3)
-HZ = 192
+REV = (1, 2, 3)
+TRANS = True
+DH1 = "v"
+ZS = 6
+VRELU = (1, 2, 3)
 CODES = "float8_e4m3fn_x4"
 WHOLE = 1.5 * 2.0 ** 23
-START = "hor0 hor1 strip p15 e0 kap e1 uoo e2 e3 kv ini coo cm4 pa nxo pb2 qu uu us half lasts cm16 x0 pk x1 d4"
-SEARCH = "g00 g01 k00 g10 g11 k01 k10 k11 p0 p1 m0 m1 s0 p2 t0 m2 s1 t1 p3 m3 s2 s3"
-MEANS = "f16 G r0 r1 r2 g0 g1 g2 g3 lt S red two X r16 s16 sc m0 O m1 o16 m2 m3 z0 z1"
+START = "zero hor0 hor1 strip p15 zeros e0 kap e1 uoo e2 e3 kv ini coo cm4 pa nxo qu pb2 uu us half lasts cm16 x0 pk x1 d4"
+SEARCH = "g01 g00 g11 g10 k00 k10 k01 k11 m0 m1 s0 t0 m2 s1 m3 s2 s3"
+MEANS = "f16 G >f r0 r1 r2 lt S red two X r16 s16 >s sc O o16 >o F p0 p1 p2 p3 rr kw g0 g1 g2 g3 m0 m1 m2 m3 z0 z1"
+AFTER = "Rm cr Cm4 Cm16 own cw pk"
 
 SCRATCH = {}
 for _n, _w, _d in (
-        ("ones", 528, "b"), ("strip", 516, "b"), ("zero", 512, "b"), ("eq", 512, "c"), ("esc", 512, "p"), ("ut", 512, "b"), ("qu", 128, "c"),
+        ("ones", 784, "b"), ("strip", 516, "b"), ("zero", 512, "b"), ("eq", 512, "c"), ("esc", 512, "p"), ("ut", 512, "b"), ("qu", 128, "c"),
         ("su", 128, "p"), ("uu", 256, "c"), ("us", 256, "p"), ("vt", 512, "b"), ("qv", 128, "c"), ("sv", 128, "p"), ("wq", 512, "c"), ("wp", 512, "p"),
         ("nxi", 16, "i"), ("coi", 16, "i"), ("nxo", 16, "u"), ("coo", 16, "u"), ("uoi", 16, "i"), ("uoo", 16, "u"), ("iot", PL, "f"), ("pif", 1, "f"),
         ("half", PL, "f"), ("m4t", 64, "b"), ("pi", 4, "i"), ("p15", 4, "i"), ("si", 4, "i"), ("kap", 4, "f"), ("kv", 4, "f"), ("ini", 4, "f"),
         ("pa", 4, "i"), ("pb", 4, "f"), ("da", 16, "b"), ("d4", 64, "b"), ("d16", 256, "b"), ("s16t", 256, "b"),
         ("fh", 4 * PL, "b"), ("sa", 256, "b"), ("sb", 256, "b"), ("hor", 8, "f"), ("sv8", 8, "f"), ("two", 8, "f"), ("sx8", 8, "f"),
         ("k1", 256, "b"), ("pk", 256, "b"), ("cm4", 256, "b"), ("cm16", 256, "b"), ("kr", 256, "b"), ("cr", 256, "b"), ("pick", 256, "f"),
-        ("kw", 16, "u"), ("cw", 16, "u"), ("junk", 512, "b"), ("jun2", 256, "f"),
-        ("ww", 2048, "f"), ("acc", 4, "f"), ("lt", 65, "b"), ("f16", 4, "u"), ("g1", 256, "b"), ("s16", 4, "u"), ("r16", 4, "u"), ("o16", 16, "u"),
-        ("rr", 128, "b"), ("byr", 64, "b"), ("byo", 64, "f"), ("zk", 256, "b"),
+        ("kw", 16, "u"), ("cw", 16, "u"), ("junk", 768, "b"), ("jun2", 256, "f"),
+        ("ww", 2048, "f"), ("acc", 4, "f"), ("lt", 65, "b"), ("g1", 256, "b"), ("r16", 4, "u"), ("mine", 32 * R, "u"), ("came", 32 * R, "u"), ("fo", 512, "b"),
+        ("rr", 128, "b"), ("rm", 128, "b"), ("byr", 64, "b"), ("byo", 64, "f"), ("zk", 256, "b"),
         ("zt", 512, "b"), ("ht", 512, "b"), ("dh", 256, "b"), ("g2", 512, "b"), ("cf", 256, "f"),
-        ("yo", 256, "f"), ("w0", 256, "b"), ("w1", 256, "b"),
-        ("zc", 128 + R * K, "c"), ("zp", 128 + R * K, "p"), ("hc", 128 + R * HZ, "c"), ("hp", 128 + R * HZ, "p")):
+        ("yo", 256, "f"), ("w0", 256, "b"), ("w1", 256, "b"), ("w2", 256, "b"),
+        ("zc", 128, "c"), ("zp", 128, "p"), ("hc", 320, "c"), ("hp", 320, "p")):
     SCRATCH[_n] = ("sbuf", [128, _w], {"b": "bfloat16", "c": CODES, "p": "uint8", "i": "int32", "u": "uint16", "f": "float32"}[_d])
 for _n in ("pf", "pw"):
     SCRATCH[_n] = ("psum", [128, 2048], "float32")
@@ -35,12 +39,13 @@ for _i in range(4):
     SCRATCH["q%d" % _i] = ("sbuf", [128, 256], CODES)
     SCRATCH["s%d" % _i] = ("sbuf", [128, 256], "uint8")
 for _i in range(R):
-    for _n in "zh":
-        SCRATCH["%sq%d" % (_n, _i)] = ("sbuf", [128, 128], CODES)
-        SCRATCH["%ss%d" % (_n, _i)] = ("sbuf", [128, 128], "uint8")
+    for _n, _w in (("h", 128), ("x", 256)):
+        SCRATCH["%sq%d" % (_n, _i)] = ("sbuf", [128, _w], CODES)
+        SCRATCH["%ss%d" % (_n, _i)] = ("sbuf", [128, _w], "uint8")
+LISTS = {"f": (0, 4), "s": (8, 4), "o": (16, 16)}
 
 DMAS = ["dx0", "dx1", "du", "dv", "dwc", "dws", "dn", "dc", "dol", "dy0", "dy1", "doc0", "doc1", "ds0", "ds1", "ds2", "ds3"]
-SEMAPHORES = ["cv", "cs", "ct", "cg", "left"] + ["za%d" % i for i in range(R)] + ["ha%d" % i for i in range(R)] + DMAS
+SEMAPHORES = ["cv", "cs", "ct", "cg", "left"] + ["%sa%d" % (_n, _i) for _n in "xfsoh" for _i in range(R)] + DMAS
 
 
 def rank_program(g, core, T, topo):
@@ -53,6 +58,7 @@ def rank_program(g, core, T, topo):
     count = {"cv": 0, "cs": 0, "ct": 0, "cg": 0, "left": 0}
     known = {q: {} for q in eng}
     wrote, read = {}, {}
+    behind = {}
 
     def over(book, reg):
         return [e for e in book.get(reg[0], []) if e[0] < reg[2] and reg[1] < e[1]]
@@ -72,12 +78,19 @@ def rank_program(g, core, T, topo):
             for e in over(read, reg):
                 if e[2] != q:
                     want[e[3]] = max(want.get(e[3], 0), e[4])
+        for s in want:
+            if any(behind.get((o, want[o]), {}).get(s, 0) >= want[s] for o in want if o != s):
+                want[s] = 0
         for s in sorted(want):
             if known[q].get(s, 0) < want[s]:
                 eng[q].wait_ge(T.sem[s], want[s])
                 known[q][s] = want[s]
+                for o, n in behind.get((s, want[s]), {}).items():
+                    known[q][o] = max(known[q].get(o, 0), n)
 
     def note(q, reads, writes, s, n):
+        if TRANS and q in known:
+            behind[(s, n)] = dict(known[q])
         for reg in writes:
             for book in (wrote, read):
                 book[reg[0]] = [e for e in book.get(reg[0], []) if not (reg[1] <= e[0] and e[1] <= reg[2])]
@@ -87,8 +100,8 @@ def rank_program(g, core, T, topo):
             book.append((reg[1], reg[2], q, s, n))
             read[reg[0]] = book
 
-    def op(q, call, reads, writes, behind=False):
-        need(q, reads, [] if behind else writes)
+    def op(q, call, reads, writes, adds=False):
+        need(q, reads, [] if adds else writes)
         s = "c" + q
         count[s] += 1
         call().then_inc(T.sem[s], 1)
@@ -152,24 +165,18 @@ def rank_program(g, core, T, topo):
                                      T[rq][:, ra:ra + n], T[rs][:, ra:ra + n], start, stop),
            [r(lq, la, la + 128), r(ls, la, la + 128), r(rq, ra, ra + n), r(rs, ra, ra + n)], [bank(buf, b)], not start)
 
-    def landing(kind, t):
-        return 128 + (K if kind == "z" else HZ) * t
-
-    def send(kind, t, peer):
-        cq, sq = kind + "q%d" % t, kind + "s%d" % t
-        need("g", [r(cq, 0, 64), r(sq, 0, 64)], [])
+    def send(sem, peer, there, a, here, c, n):
+        need("g", [r(here, c, c + n)], [])
         dst = T.cores[peer]
         rid, pid, _se = topo.addr(dst)
-        m, arr = topo.mask(core, dst), T.sem[kind + "a%d" % t]
-        a = landing(kind, t)
-        g.remote_dma(T[kind + "c"][:, a:a + K].bitcast(dt.uint8), T[cq][:, 0:64].bitcast(dt.uint8), arr, T.sem.left, pid, rid, m)
-        g.remote_dma(T[kind + "p"][:, a:a + K], T[sq][:, 0:64], arr, T.sem.left, pid, rid, m)
-        count["left"] += 2 * len(topo.engines(core, dst))
+        o, i = T[there][:, a:a + n], T[here][:, c:c + n]
+        if SCRATCH[here][2] == CODES:
+            o, i = o.bitcast(dt.uint8), i.bitcast(dt.uint8)
+        g.remote_dma(o, i, T.sem[sem], T.sem.left, pid, rid, topo.mask(core, dst))
+        count["left"] += len(topo.engines(core, dst))
 
-    def arrival(kind, t, peer):
-        n = 2 * len(topo.engines(T.cores[peer], core))
-        a = landing(kind, t)
-        note("r", [], [(kind + "c", a, a + K), (kind + "p", a, a + K)], kind + "a%d" % t, n)
+    def arrival(sem, peer, calls, regions):
+        note("r", [], regions, sem, calls * len(topo.engines(T.cores[peer], core)))
 
     def picker(name, slots, n, run, col):
         q = T.kap[:, 0:1]
@@ -181,10 +188,11 @@ def rank_program(g, core, T, topo):
         horner(T.pick[:, 0:256], T.d16[:, 0:256], T[row][:, 0:256], 0.0, [r("d16"), r(row)], [r("pick")])
         ts(T[dest][:, 0:16], T.pick[:, 15:256:16], T.pb[:, 1:2], base, mult, add, [r("pick"), r("pb", 1, 2)], [r(dest)])
 
-    def prekeys_own():
-        for h in range(2):
-            a, e = 128 * h, 128 * h + 128
-            ts(T.cm16[:, a:e], T.cm4[:, a:e], 4.0, 2.0 - h, mult, add, [r("cm4")], [r("cm16", a, e)])
+    def prekeys_own(on="v"):
+        if on == "s":
+            act(T.cm16[:, 0:256], T.cm4[:, 0:256], F.Copy, [r("cm4")], [r("cm16")], scale=4.0, bias=1.0)
+        else:
+            ts(T.cm16[:, 0:256], T.cm4[:, 0:256], 4.0, 1.0, mult, add, [r("cm4")], [r("cm16")])
 
     def prekeys_next():
         tt(T.pk[:, 0:256], T.cm4[:, 0:256].indirect(T.nxo[:, 0:16]), T.cm16[:, 0:256], add, [r("cm4"), r("nxo"), r("cm16")], [r("pk")])
@@ -202,16 +210,25 @@ def rank_program(g, core, T, topo):
     whole("m4t", 0, 64, [[0, 16], [4, 4]])
     whole("uoi", 0, 16, [[1, 2], [16, 8]])
     whole("iot", 128, PL, [[1, PL - 128]], 128)
-    whole("ones", 16, 528, [[0, 512]], 1)
+    whole("ones", 16, 16 + 256 * REV[0], [[0, 256 * REV[0]]], 1)
+    whole("ones", 15, 16, [[0, 1]])
+    for b in range(4):
+        whole("fh", PL * b + C, PL * b + PL, [[0, PL - C]])
+
+    def zeros():
+        for name, a, b in (("zt", 256, 512), ("byr", 0, 64), ("two", 0, 8)):
+            act(T[name][:, a:b], T.zero[:, 0:b - a], F.Copy, [r("zero")], [r(name, a, b)])
 
     def const(b):
         op("v", lambda: V.quantize_mx(T.eq[:, 128 * b:128 * b + 128], T.esc[:, 128 * b:128 * b + 128], T.strip[:, 3 - b:515 - b]),
            [r("strip")], [r("eq", 128 * b, 128 * b + 128), r("esc", 128 * b, 128 * b + 128)])
 
     def lasts():
-        for i in range(2):
+        for i in range(REV[0]):
             act(T.ones[:, 271 + 256 * i:272 + 256 * i], T.ini[:, i:i + 1], F.Copy, [r("ini")], [r("ones", 271 + 256 * i, 272 + 256 * i)])
     steps = {
+        "zero": lambda: fill("zero", 0, 512, 0.0),
+        "zeros": zeros,
         "hor0": lambda: fill("hor", 0, 8, 0.0, 2),
         "hor1": lambda: fill("hor", 1, 8, -1023.0 / 1024.0, 2),
         "strip": lambda: ts(T.strip[:, 3:515:4], T.iot[:, 0:128], T.pif[:, 0:1], None, AluOpType.is_equal, None,
@@ -245,30 +262,40 @@ def rank_program(g, core, T, topo):
     need("y", [r("t0")], [])
     dma("y", "dwc", T.wq[:, 0:512].bitcast(dt.uint8), T.wc[:, 0:2048], [], [r("wq")])
     dma("y", "dws", T.wp[:, 0:512], T.ws[:, 0:512], [], [r("wp")])
-    dma("y", "dv", T.vt[:], T.v[:], [], [r("vt")])
-    whole("ones", 15, 16, [[0, 1]])
-    whole("lt", 64, 65, [[0, 1]], -64)
-    for b in range(4):
-        whole("fh", PL * b + C, PL * b + PL, [[0, PL - C]])
-    whole("two", 0, 8, [[0, 8]])
-    whole("zt", 256, 512, [[0, 256]])
-    whole("byr", 0, 64, [[0, 64]])
-    whole("s16t", 0, 256, [[0, 16], [1, 16]])
-    whole("rr", 0, 128, [[0, 128]])
 
     for t in range(R):
-        q, s = "q%d" % t, "s%d" % t
+        q, s, xq, xs = "q%d" % t, "s%d" % t, "xq%d" % t, "xs%d" % t
         to, frm = (rank + STEP[t]) % len(T.cores), (rank - STEP[t]) % len(T.cores)
+        for h in range(2):
+            send("xa%d" % t, to, xq, 128 * h, q, 128 * h, 128)
+        send("xa%d" % t, to, xs, 0, s, 0, C)
+        arrival("xa%d" % t, frm, 3, [r(xq), r(xs)])
+        if t == 0:
+            whole("lt", 64, 65, [[0, 1]], -64)
+            whole("s16t", 0, 256, [[0, 16], [1, 16]])
+            for name, a, b in (("rr", 0, 128), ("rm", 0, 128), ("ht", 256, 512)):
+                whole(name, a, b, [[0, b - a]])
+
+        def lst(buf, k):
+            a = 32 * t + LISTS[k][0]
+            return T[buf][:, a:a + LISTS[k][1]], r(buf, a, a + LISTS[k][1])
+
+        def send_list(k):
+            a = 32 * t + LISTS[k][0]
+            send("%sa%d" % (k, t), to, "came", a, "mine", a, LISTS[k][1])
+            arrival("%sa%d" % (k, t), frm, 1, [lst("came", k)[1]])
+
+        def unpack(cq, sq):
+            for b in range(4):
+                mm(b, "pf", 256, "eq", "esc", 128 * b, cq, sq, 0)
         for h in range(2):
             for k in range(2):
                 mm(2 * h + k, "pw", 128, "uu", "us", 128 * k, q, s, 128 * h)
-        for b in range(4):
-            mm(b, "pf", 256, "eq", "esc", 128 * b, q, s, 0)
 
         def sign(h, k):
             n, a, e = ("sa", "sb")[k], 128 * h, 128 * h + 128
             i = T.pw[:, 1024 * h + 512 * k:1024 * h + 512 * k + 128]
-            if (h, k) == (1, 0):
+            if k == 0:
                 ts(T[n][:, a:e], i, 0.0, 2.0, AluOpType.is_lt, mult, [bank("pw", 2 * h + k)], [r(n, a, e)])
             else:
                 act(T[n][:, a:e], i, F.Sign, [bank("pw", 2 * h + k)], [r(n, a, e)], bias=-1e-36, scale=-1.0)
@@ -280,8 +307,8 @@ def rank_program(g, core, T, topo):
             else:
                 tt(T.kr[:, a:e], T.k1[:, a:e], T.sb[:, a:e], mult, [r("k1", a, e), r("sb", a, e)], [r("kr", a, e)])
 
-        def plane(b):
-            act(T.fh[:, PL * b:PL * b + C], T.pf[:, 512 * b:512 * b + C], F.Copy, [bank("pf", b)], [r("fh", PL * b, PL * b + C)])
+        def plane(b, on):
+            copy(on, T.fh[:, PL * b:PL * b + C], T.pf[:, 512 * b:512 * b + C], [bank("pf", b)], [r("fh", PL * b, PL * b + C)])
 
         def mask(i):
             ts(T["m%d" % i][:, 0:256], T.kr[:, 0:256], T.kv[:, i:i + 1], 2.0 ** -10, AluOpType.not_equal, amax,
@@ -301,94 +328,118 @@ def rank_program(g, core, T, topo):
             a = 512 * i + 256
             act(T.junk[:, 256 * i:256 * i + 256], T["w%d" % i][:, 0:256], F.Copy, [r("w%d" % i)],
                 [r("junk", 256 * i, 256 * i + 256), r("ww", a, a + 1)], accum_out=T.ww[:, a:a + 1])
-        steps = {"g": sign, "k": key, "p": plane, "m": mask, "s": scan, "t": total}
+        steps = {"g": sign, "k": key, "m": mask, "s": scan, "t": total, "F": lambda: unpack(xq, xs), "p": lambda b: plane(b, "s")}
         for w in SEARCH.split():
             steps[w[0]](*[int(ch) for ch in w[1:]])
 
         vv, rv = T.ww[:, 256:2048:512], [r("ww", 512 * i + 256, 512 * i + 257) for i in range(4)]
         rg = [r("ww", 512 * i, 512 * i + 1) for i in range(4)]
-        row, rrow = T.half[:, 0:PL].indirect(T.f16[:, 0:4]), [r("half"), r("f16")]
+        (f16, rf), (s16, rs), (o16, ro) = [lst("mine", k) for k in "fso"]
+        (fin, rfin), (sin, rsin), (oin, roin) = [lst("came", k) for k in "fso"]
+        row, rrow = T.half[:, 0:PL].indirect(f16), [r("half"), rf]
+        crow = "cr" if t < R - 1 else "cf"
 
         def rank_of_key(i):
             act(T.jun2[:, 64 * i:64 * i + 64], row, F.Sign, rrow + [rv[i]], [r("jun2", 64 * i, 64 * i + 64), r("acc", i, i + 1)],
                 bias=T.ww[:, 512 * i + 256:512 * i + 257], scale=-1.0, accum_out=T.acc[:, i:i + 1])
 
         def first(b, on):
-            copy(on, T.g1[:, 64 * b:64 * b + 64], T.fh[:, PL * b:PL * b + PL].indirect(T.f16[:, 0:4]),
-                 [r("fh", PL * b, PL * b + PL), r("f16")], [r("g1", 64 * b, 64 * b + 64)])
+            copy(on, T.g1[:, 64 * b:64 * b + 64], T.fh[:, PL * b:PL * b + PL].indirect(fin),
+                 [r("fh", PL * b, PL * b + PL), rfin], [r("g1", 64 * b, 64 * b + 64)])
 
         def mean(b):
-            tt(T.zk[:, 64 * b:64 * b + 64], T.fh[:, PL * b:PL * b + PL].indirect(T.s16[:, 0:4]), T.g1[:, 64 * b:64 * b + 64], add,
-               [r("fh", PL * b, PL * b + PL), r("s16"), r("g1", 64 * b, 64 * b + 64)], [r("zk", 64 * b, 64 * b + 64)])
+            tt(T.zk[:, 64 * b:64 * b + 64], T.fh[:, PL * b:PL * b + PL].indirect(sin), T.g1[:, 64 * b:64 * b + 64], add,
+               [r("fh", PL * b, PL * b + PL), rsin, r("g1", 64 * b, 64 * b + 64)], [r("zk", 64 * b, 64 * b + 64)])
 
         def final(h):
-            o, i, rd, wr = T.zt[:, 128 * h:128 * h + 128], T.zk[:, 0:256].indirect(T.o16[:, 8 * h:8 * h + 8]), \
-                [r("zk"), r("o16")], [("zt", 128 * h, 128 * h + 128)]
+            a, e = ((0, ZS), (ZS, 16))[h]
+            o, i, rd, wr = T.zt[:, 16 * a:16 * e], T.zk[:, 0:256].indirect(T.came[:, roin[1] + a:roin[1] + e]), \
+                [r("zk"), roin], [("zt", 16 * a, 16 * e)]
             if h == 0:
                 act(o, i, F.Copy, rd, wr, scale=0.5)
             else:
                 ts(o, i, 0.5, None, mult, None, rd, wr)
+
+        def ranks_row():
+            if t == 0:
+                picker("d16", "s16t", 256, 16, 1)
+            ts(T.rr[:, 0:128:2], T.half[:, 0:64].indirect(T.r16[:, 0:4]), -0.5, None, add, None, [r("half"), r("r16")], [r("rr")])
+
+        def own():
+            unpack(q, s)
+            for b in range(2):
+                act(T.fo[:, C * b:C * b + C], T.pf[:, 512 * b:512 * b + C], F.Copy, [bank("pf", b)], [r("fo", C * b, C * b + C)])
         steps = {
-            "f16": lambda: cp(T.f16[:, 0:4], vv, rv, [r("f16")]),
+            "f16": lambda: cp(f16, vv, rv, [rf]),
             "two": lambda: ts(T.two[:, 0:8:2], T.sv8[:, 1:8:2], 0.25, 1024.0, AluOpType.is_lt, mult, [r("sv8")], [r("two")]),
             "X": lambda: op("v", lambda: V.tensor_tensor_scan(T.sx8[:, 7::-1], T.two[:, 7::-1], T.sv8[:, 7::-1], 0.0, mult, amax),
                             [r("two"), r("sv8")], [r("sx8")]),
             "G": lambda: ts(T.ww[:, 0:2048:512], vv, WHOLE, -WHOLE, add, add, rv, rg),
             "S": lambda: horner(T.sv8[:, 0:8], T.hor[:, 0:8], T.ww[:, 0:2048:256], 0.0, [r("hor")] + rv + rg, [r("sv8")]),
-            "s16": lambda: ts(T.s16[:, 0:4], T.sx8[:, 0:8:2], 0.0625, None, add, None, [r("sx8")], [r("s16")]),
+            "s16": lambda: ts(s16, T.sx8[:, 0:8:2], 0.0625, None, add, None, [r("sx8")], [rs]),
             "lt": lambda: ts(T.lt[:, 0:64], row, T.ww[:, 1792:1793], 2.0, AluOpType.is_lt, mult, rrow + [rv[3]], [r("lt", 0, 64)]),
             "red": lambda: op("v", lambda: V.tensor_reduce(T.acc[:, 3:4], T.lt[:, 0:65], AxisListType.X, add), [r("lt")], [r("acc", 3, 4)]),
             "r16": lambda: ts(T.r16[:, 0:4], T.acc[:, 0:4], 0.5, 32.0, mult, add, [r("acc")], [r("r16")]),
             "sc": lambda: cp(T.byr[:, 0:64].indirect(T.r16[:, 0:4]), T.iot[:, 0:64], [r("iot"), r("r16")], [r("byr")]),
             "O": lambda: horner(T.byo[:, 0:64], T.d4[:, 0:64], T.byr[:, 0:64], 0.0, [r("d4"), r("byr")], [r("byo")]),
-            "o16": lambda: ts(T.o16[:, 0:16], T.byo[:, 3:64:4], T.pb[:, 0:1], T.pb[:, 2:3], mult, add, [r("byo"), r("pb", 0, 3)], [r("o16")]),
+            "o16": lambda: ts(o16, T.byo[:, 3:64:4], T.pb[:, 0:1], T.pb[:, 2:3], mult, add, [r("byo"), r("pb", 0, 3)], [ro]),
+            "F": lambda: unpack(xq, xs),
+            "rr": ranks_row,
+            "kw": lambda: as_list("kr", "kw", 63.25),
+            "cr": lambda: cp(T[crow][:, 0:256], T.rr[:, 0:128].indirect(T.kw[:, 0:16]), [r("rr"), r("kw")], [r(crow)]),
+            "Cr": lambda: act(T[crow][:, 0:256], T.rr[:, 0:128].indirect(T.kw[:, 0:16]), F.Copy, [r("rr"), r("kw")], [r(crow)]),
+            "cw": lambda: as_list(crow, "cw", 0.125),
+            "own": own,
+            "rm": lambda: cp(T.rm[:, 0:128:2], T.m4t[:, 0:64].indirect(T.r16[:, 0:4]), [r("m4t"), r("r16")], [r("rm")]),
+            "cm4": lambda: copy("v", T.cm4[:, 0:256], T.rm[:, 0:128].indirect(T.kw[:, 0:16]), [r("rm"), r("kw")], [r("cm4")]),
+            "Cm4": lambda: copy("s", T.cm4[:, 0:256], T.rm[:, 0:128].indirect(T.kw[:, 0:16]), [r("rm"), r("kw")], [r("cm4")]),
+            "cm16": prekeys_own,
+            "Cm16": lambda: prekeys_own("s"),
+            "Rm": lambda: copy("s", T.rm[:, 0:128:2], T.m4t[:, 0:64].indirect(T.r16[:, 0:4]), [r("m4t"), r("r16")], [r("rm")]),
+            "pk": prekeys_next,
         }
+        for k in "fso":
+            steps[">" + k] = lambda k=k: send_list(k)
         for i in range(4):
             steps["r%d" % i] = lambda i=i: rank_of_key(i)
             steps["g%d" % i] = lambda i=i: first(i, "s")
             steps["v%d" % i] = lambda i=i: first(i, "v")
             steps["m%d" % i] = lambda i=i: mean(i)
             steps["z%d" % i] = lambda i=i: final(i)
+            steps["p%d" % i] = lambda i=i: plane(i, "s")
+            steps["P%d" % i] = lambda i=i: plane(i, "v")
         for w in MEANS.split():
-            steps[w]()
-        quant("zq%d" % t, "zs%d" % t, "zt", 0, 128)
-        send("z", t, to)
-        arrival("z", t, frm)
-        if t == 0:
-            fill("zero", 0, 512, 0.0)
-            picker("d16", "s16t", 256, 16, 1)
-            quant("zc", "zp", "zero", 0, 128)
-            fill("ht", 256, 512, 0.0)
-        ts(T.rr[:, 0:128:2], T.half[:, 0:64].indirect(T.r16[:, 0:4]), -0.5, None, add, None, [r("half"), r("r16")], [r("rr")])
-        as_list("kr", "kw", 63.25)
-        crow = "cr" if t < R - 1 else "cf"
-        cp(T[crow][:, 0:256], T.rr[:, 0:128].indirect(T.kw[:, 0:16]), [r("rr"), r("kw")], [r(crow)])
-        as_list(crow, "cw", 0.125)
+            if t < R - 1 or w.lower() not in ("rm", "cm4", "cm16", "pk"):
+                steps[w]()
+        quant("zc", "zp", "zt", 0, 128)
         for b in range(4):
-            mm(b, "pw", 128, "wq", "wp", 128 * b, "zc", "zp", 64 + K * t)
+            mm(b, "pw", 128, "wq", "wp", 128 * b, "zc", "zp", 0)
         for b in range(4):
-            o, i, rd, wr = T.ht[:, b:256:4], T.pw[:, 512 * b + 64:512 * b + 128], [bank("pw", b)], [("ht", 64 * b, 64 * b + 64)]
-            if b in (1, 3):
+            o, i, rd, wr = T.ht[:, b:256:4], T.pw[:, 512 * b:512 * b + 64], [bank("pw", b)], [("ht", 64 * b, 64 * b + 64)]
+            if b in VRELU:
                 ts(o, i, 0.0, 0.03125, amax, mult, rd, wr)
             else:
                 act(o, i, F.Relu, rd, wr, scale=0.03125)
         quant("hq%d" % t, "hs%d" % t, "ht", 0, 128)
-        send("h", t, frm)
-        arrival("h", t, to)
+        land = 128
+        send("ha%d" % t, frm, "hc", land, "hq%d" % t, 0, K)
+        send("ha%d" % t, frm, "hp", land, "hs%d" % t, 0, K)
+        arrival("ha%d" % t, to, 2, [r("hc", land, land + K), r("hp", land, land + K)])
         if t == 0:
-            for k in range(R + 1):
-                quant("hc", "hp", "zero", HZ * k, 128)
-        if t < R - 1:
-            cp(T.cm4[:, 0:256], T.m4t[:, 0:64].indirect(T.cw[:, 0:16]), [r("m4t"), r("cw")], [r("cm4")])
-            prekeys_own()
-            prekeys_next()
-        else:
+            need("y", [r("zc")], [])
+            dma("y", "dv", T.vt[:], T.v[:], [], [r("vt")])
+            for a in (0, 192):
+                quant("hc", "hp", "zero", a, 128)
+        for w in AFTER.split():
+            if t < R - 1 or w.lower() not in ("rm", "cm4", "cm16", "pk"):
+                steps[w]()
+        if t == R - 1:
             dma("y", "dol", T.ol[:], T.cf[0:128:16, 0:256], [r("cf")], [])
             quant("qv", "sv", "vt", 0, 128)
         new = "t%d" % (t + 1)
         for b in range(4):
-            mm(min(b, 2), "pw", 128, "eq", "esc", 128 * b, "hc", "hp", landing("h", t) - 64 * (b == 3), b != 3, b != 2)
-        for b, n, on in ((0, 64, "v"), (1, 64, "s"), (2, 128, "s")):
+            mm(min(b, 2), "pw", 128, "eq", "esc", 128 * b, "hc", "hp", land - 64 * (b == 3), b != 3, b != 2)
+        for b, n, on in ((0, 64, "v"), (1, 64, DH1), (2, 128, "s")):
             copy(on, T.dh[:, 64 * b:64 * b + n], T.pw[:, 512 * b:512 * b + n], [bank("pw", b)], [r("dh", 64 * b, 64 * b + n)])
         for h in range(2):
             for b in (2, 3):
@@ -396,8 +447,8 @@ def rank_program(g, core, T, topo):
                 act(T.g2[:, o:o + 128], T.dh[:, 64 * b:64 * b + 64].indirect(T.cw[:, 8 * h:8 * h + 8]), F.Copy,
                     [r("dh", 64 * b, 64 * b + 64), r("cw")], [r("g2", o, o + 128)])
         for b in (0, 1):
-            tt(T[new][:, b:1024:4], T.dh[:, 64 * b:64 * b + 64].indirect(T.cw[:, 0:16]), T.fh[:, PL * b:PL * b + C], add,
-               [r("dh", 64 * b, 64 * b + 64), r("cw"), r("fh", PL * b, PL * b + C)], [(new, C * b, C * b + C)])
+            tt(T[new][:, b:1024:4], T.dh[:, 64 * b:64 * b + 64].indirect(T.cw[:, 0:16]), T.fo[:, C * b:C * b + C], add,
+               [r("dh", 64 * b, 64 * b + 64), r("cw"), r("fo", C * b, C * b + C)], [(new, C * b, C * b + C)])
         for h in range(2):
             for b in (2, 3):
                 o, p, w = C * (b - 2) + 128 * h, 512 * b + 128 * h, C * b + 128 * h

@@ -3,17 +3,26 @@ from concourse.mybir import dt, AluOpType, AxisListType, ActivationFunctionType
 C, K, R = 256, 64, 3
 STEP = [1, 2, 4]
 PL = C + 16 + K
-REV = (1, 2, 3)
+REV = (2, 3)
 TRANS = True
+UP = False
+VS = (0, 1)
+HALF = 0
+VR = 0
+TAIL = 0
 DH1 = "v"
-ZS = 6
-VRELU = (1, 2, 3)
+ZS = 8
+VRELU = (2, 3)
 CODES = "float8_e4m3fn_x4"
 WHOLE = 1.5 * 2.0 ** 23
-START = "zero hor0 hor1 strip p15 zeros e0 kap e1 uoo e2 e3 kv ini coo cm4 pa nxo qu pb2 uu us half lasts cm16 x0 pk x1 d4"
-SEARCH = "g01 g00 g11 g10 k00 k10 k01 k11 m0 m1 s0 t0 m2 s1 m3 s2 s3"
-MEANS = "f16 G >f r0 r1 r2 lt S red two X r16 s16 >s sc O o16 >o F p0 p1 p2 p3 rr kw g0 g1 g2 g3 m0 m1 m2 m3 z0 z1"
-AFTER = "Rm cr Cm4 Cm16 own cw pk"
+START = "blanks strip p15 e0 kap e1 kv ini uoo e2 coo cm4 qu e3 uu us lasts half hor x0 nxo cm16 pa pk x1"
+SEARCH = "g01 g00 +d16 k00 g11 g10 k01 x30 x20 y30 k10 m00 k11 x31 y20 y31 m10 m01 m11 own s0 t0 m21 s1 t1 s2 s3 +da"
+MEANS = "f16 G >f r0 r1 r2 lt S red two +pb2 X r16 s16 >s sc +u4 O o16 >o +u16 +zero F2 p20 p21 p22 p23 g0 g1 g2 g3 Rr kw m0 m1 m2 m3 z0 z1"
+AFTER = "+z0 +z1 Rm cr Cm4 Cm16 o0 o1 cw pk"
+EXPAND = "d0 d1 D2 G20 G30 G21 G31 b0 b1 a20 a30 a21 q0 a31 q1"
+LOADS = "yu yx0 yx1 sc sn"
+OWN = 512
+PICK = "b"
 
 SCRATCH = {}
 for _n, _w, _d in (
@@ -21,11 +30,11 @@ for _n, _w, _d in (
         ("su", 128, "p"), ("uu", 256, "c"), ("us", 256, "p"), ("vt", 512, "b"), ("qv", 128, "c"), ("sv", 128, "p"), ("wq", 512, "c"), ("wp", 512, "p"),
         ("nxi", 16, "i"), ("coi", 16, "i"), ("nxo", 16, "u"), ("coo", 16, "u"), ("uoi", 16, "i"), ("uoo", 16, "u"), ("iot", PL, "f"), ("pif", 1, "f"),
         ("half", PL, "f"), ("m4t", 64, "b"), ("pi", 4, "i"), ("p15", 4, "i"), ("si", 4, "i"), ("kap", 4, "f"), ("kv", 4, "f"), ("ini", 4, "f"),
-        ("pa", 4, "i"), ("pb", 4, "f"), ("da", 16, "b"), ("d4", 64, "b"), ("d16", 256, "b"), ("s16t", 256, "b"),
+        ("pa", 4, "i"), ("pb", 4, "f"), ("da", 16, "b"), ("fr", 64, "f"), ("lt4", 256, "b"), ("d64", 256, "b"), ("ac4", 256, "b"), ("d16", 256, "b"), ("s16t", 256, "b"),
         ("fh", 4 * PL, "b"), ("sa", 256, "b"), ("sb", 256, "b"), ("hor", 8, "f"), ("sv8", 8, "f"), ("two", 8, "f"), ("sx8", 8, "f"),
-        ("k1", 256, "b"), ("pk", 256, "b"), ("cm4", 256, "b"), ("cm16", 256, "b"), ("kr", 256, "b"), ("cr", 256, "b"), ("pick", 256, "f"),
+        ("k1", 256, "b"), ("pk", 256, "b"), ("cm4", 256, "b"), ("cm16", 256, "b"), ("kr", 256, "b"), ("cr", 256, "b"), ("pick", 256, PICK),
         ("kw", 16, "u"), ("cw", 16, "u"), ("junk", 768, "b"), ("jun2", 256, "f"),
-        ("ww", 2048, "f"), ("acc", 4, "f"), ("lt", 65, "b"), ("g1", 256, "b"), ("r16", 4, "u"), ("mine", 32 * R, "u"), ("came", 32 * R, "u"), ("fo", 512, "b"),
+        ("ww", 2048, "f"), ("acc", 4, "f"), ("lt", 65, "b"), ("lu", 65, "b"), ("fu", 4, "u"), ("gs", 256, "b"), ("sg", 512, "b"), ("g1", 256, "b"), ("r16", 4, "u"), ("mine", 32 * R, "u"), ("came", 32 * R, "u"), ("fo", 1024, "b"),
         ("rr", 128, "b"), ("rm", 128, "b"), ("byr", 64, "b"), ("byo", 64, "f"), ("zk", 256, "b"),
         ("zt", 512, "b"), ("ht", 512, "b"), ("dh", 256, "b"), ("g2", 512, "b"), ("cf", 256, "f"),
         ("yo", 256, "f"), ("w0", 256, "b"), ("w1", 256, "b"), ("w2", 256, "b"),
@@ -44,8 +53,8 @@ for _i in range(R):
         SCRATCH["%ss%d" % (_n, _i)] = ("sbuf", [128, _w], "uint8")
 LISTS = {"f": (0, 4), "s": (8, 4), "o": (16, 16)}
 
-DMAS = ["dx0", "dx1", "du", "dv", "dwc", "dws", "dn", "dc", "dol", "dy0", "dy1", "doc0", "doc1", "ds0", "ds1", "ds2", "ds3"]
-SEMAPHORES = ["cv", "cs", "ct", "cg", "left"] + ["%sa%d" % (_n, _i) for _n in "xfsoh" for _i in range(R)] + DMAS
+DMAS = ["dx0", "dx1", "du", "dv", "dwc", "dws", "dn", "dc", "dol", "doc0", "dy0", "doc1", "ds0", "ds1", "ds2", "ds3", "dy1"]
+SEMAPHORES = ["cv", "cs", "ct", "cg", "left"] + ["%sa%d" % (_n, _i) for _n in "xyfsoh" for _i in range(R)] + DMAS
 
 
 def rank_program(g, core, T, topo):
@@ -83,6 +92,8 @@ def rank_program(g, core, T, topo):
                 want[s] = 0
         for s in sorted(want):
             if known[q].get(s, 0) < want[s]:
+                if UP and s == "c" + q:
+                    want[s] = max(want[s], count[s] - 1)
                 eng[q].wait_ge(T.sem[s], want[s])
                 known[q][s] = want[s]
                 for o, n in behind.get((s, want[s]), {}).items():
@@ -106,6 +117,30 @@ def rank_program(g, core, T, topo):
         count[s] += 1
         call().then_inc(T.sem[s], 1)
         note(q, reads, writes, s, count[s])
+
+    def ahead(w):
+        q, s = w[1], "c" + w[2]
+        if known[q].get(s, 0) < count[s]:
+            eng[q].wait_ge(T.sem[s], count[s])
+            known[q][s] = count[s]
+            for o, n in behind.get((s, count[s]), {}).items():
+                known[q][o] = max(known[q].get(o, 0), n)
+
+    setup = {}
+
+    def run(order, steps, skip=()):
+        for w in order.split():
+            if w[0] == "^":
+                ahead(w)
+            elif w[0] == "+":
+                if w[1:] in setup:
+                    setup.pop(w[1:])()
+            elif w.lower() in skip:
+                continue
+            elif w in steps:
+                steps[w]()
+            else:
+                steps[w[0]](*[int(ch) for ch in w[1:]])
 
     def dma(q, s, out, in_, reads, writes):
         need(q, reads, writes)
@@ -178,59 +213,67 @@ def rank_program(g, core, T, topo):
     def arrival(sem, peer, calls, regions):
         note("r", [], regions, sem, calls * len(topo.engines(T.cores[peer], core)))
 
-    def picker(name, slots, n, run, col):
-        q = T.kap[:, 0:1]
-        ts(T[name][:, 0:n], T[slots][:, 0:n], q, 256.0, AluOpType.is_gt, mult, [r(slots), r("kap")], [r(name)])
-        ts(T.da[:, 0:run], T[slots][:, 0:run], q, 2.0 ** -8, AluOpType.is_le, amax, [r(slots), r("kap")], [r("da")])
-        op("v", lambda: V.tensor_reduce(T.pb[:, col:col + 1], T.da[:, 0:run], AxisListType.X, mult), [r("da")], [r("pb", col, col + 1)])
+    def undo(col, step):
+        op("v", lambda: V.tensor_reduce(T.pb[:, col:col + 1], T.da[:, 0:16:step], AxisListType.X, mult), [r("da")], [r("pb", col, col + 1)])
 
     def as_list(row, dest, base):
         horner(T.pick[:, 0:256], T.d16[:, 0:256], T[row][:, 0:256], 0.0, [r("d16"), r(row)], [r("pick")])
         ts(T[dest][:, 0:16], T.pick[:, 15:256:16], T.pb[:, 1:2], base, mult, add, [r("pick"), r("pb", 1, 2)], [r(dest)])
 
     def prekeys_own(on="v"):
-        if on == "s":
-            act(T.cm16[:, 0:256], T.cm4[:, 0:256], F.Copy, [r("cm4")], [r("cm16")], scale=4.0, bias=1.0)
-        else:
-            ts(T.cm16[:, 0:256], T.cm4[:, 0:256], 4.0, 1.0, mult, add, [r("cm4")], [r("cm16")])
+        for a, e in ((0, 128), (128, C)) if len(VS) == 1 else ((0, C),):
+            bias = 1.0 if a // 128 in VS else 2.0
+            if on == "s":
+                act(T.cm16[:, a:e], T.cm4[:, a:e], F.Copy, [r("cm4")], [r("cm16", a, e)], scale=4.0, bias=bias)
+            else:
+                ts(T.cm16[:, a:e], T.cm4[:, a:e], 4.0, bias, mult, add, [r("cm4")], [r("cm16", a, e)])
 
     def prekeys_next():
         tt(T.pk[:, 0:256], T.cm4[:, 0:256].indirect(T.nxo[:, 0:16]), T.cm16[:, 0:256], add, [r("cm4"), r("nxo"), r("cm16")], [r("pk")])
 
-    dma("y", "du", T.ut[:], T.u[:], [], [r("ut")])
+    loads = {"u": (T.ut[:], T.u[:], r("ut")), "c": (T.coi[:], T.co[:], r("coi")), "n": (T.nxi[:], T.nx[:], r("nxi"))}
     for h in range(2):
-        dma("y", "dx%d" % h, T.t0[:, 512 * h:512 * h + 512], T.x[:, 512 * h:512 * h + 512], [], [r("t0", 512 * h, 512 * h + 512)])
-    dma("s", "dc", T.coi[:], T.co[:], [], [r("coi")])
-    dma("s", "dn", T.nxi[:], T.nx[:], [], [r("nxi")])
+        loads["x%d" % h] = (T.t0[:, 512 * h:512 * h + 512], T.x[:, 512 * h:512 * h + 512], r("t0", 512 * h, 512 * h + 512))
+    for w in LOADS.split():
+        dma(w[0], "d" + w[1:], loads[w[1:]][0], loads[w[1:]][1], [], [loads[w[1:]][2]])
     fill("strip", 0, 516, 0.0)
     whole("pif", 0, 1, [[0, 1]], 0, 1)
     whole("iot", 0, 128, [[1, 128]])
     whole("pi", 0, 4, [[0, 4]], 0, 1)
     whole("si", 0, 4, [[16, 4]])
-    whole("m4t", 0, 64, [[0, 16], [4, 4]])
     whole("uoi", 0, 16, [[1, 2], [16, 8]])
-    whole("iot", 128, PL, [[1, PL - 128]], 128)
-    whole("ones", 16, 16 + 256 * REV[0], [[0, 256 * REV[0]]], 1)
+    whole("m4t", 0, 64, [[0, 16], [4, 4]])
+    fill("ones", 16, 16 + 256 * REV[0], 1.0)
     whole("ones", 15, 16, [[0, 1]])
-    for b in range(4):
-        whole("fh", PL * b + C, PL * b + PL, [[0, PL - C]])
+    whole("iot", 128, PL, [[1, PL - 128]], 128)
+    whole("sx8", 0, 8, [[0, 4], [-1023, 2]])
+    whole("s16t", 0, 256, [[0, 16], [1, 16]])
 
-    def zeros():
-        for name, a, b in (("zt", 256, 512), ("byr", 0, 64), ("two", 0, 8)):
-            act(T[name][:, a:b], T.zero[:, 0:b - a], F.Copy, [r("zero")], [r(name, a, b)])
+    def blanks():
+        for b in range(4):
+            act(T.fh[:, PL * b + C:PL * b + PL], T.iot[:, 0:PL - C], F.Copy, [r("iot", 0, PL - C)], [r("fh", PL * b + C, PL * b + PL)], scale=0.0)
+
+    def zeros(*runs):
+        for name, a, b in runs:
+            whole(name, a, b, [[0, b - a]])
 
     def const(b):
         op("v", lambda: V.quantize_mx(T.eq[:, 128 * b:128 * b + 128], T.esc[:, 128 * b:128 * b + 128], T.strip[:, 3 - b:515 - b]),
            [r("strip")], [r("eq", 128 * b, 128 * b + 128), r("esc", 128 * b, 128 * b + 128)])
 
+    def factors():
+        act(T.pb[:, 3:4], T.kap[:, 0:1], F.Copy, [r("kap")], [r("pb", 3, 4)], scale=-1.0, bias=-0.5)
+        act(T.pick[:, 0:256], T.s16t[:, 0:256], F.Sign, [r("s16t"), r("pb", 3, 4)], [r("pick")], bias=T.pb[:, 3:4])
+        act(T.da[:, 0:16], T.pick[:, 0:16], F.Copy, [r("pick")], [r("da")], scale=-255.0 / 512.0, bias=257.0 / 512.0)
+        act(T.d16[:, 0:256], T.pick[:, 0:256], F.Relu, [r("pick")], [r("d16")], scale=256.0)
+
     def lasts():
         for i in range(REV[0]):
             act(T.ones[:, 271 + 256 * i:272 + 256 * i], T.ini[:, i:i + 1], F.Copy, [r("ini")], [r("ones", 271 + 256 * i, 272 + 256 * i)])
     steps = {
-        "zero": lambda: fill("zero", 0, 512, 0.0),
-        "zeros": zeros,
-        "hor0": lambda: fill("hor", 0, 8, 0.0, 2),
-        "hor1": lambda: fill("hor", 1, 8, -1023.0 / 1024.0, 2),
+        "hor": lambda: act(T.hor[:, 0:8], T.sx8[:, 0:8], F.Copy, [r("sx8")], [r("hor")], scale=2.0 ** -10),
+        "Cm16": lambda: prekeys_own("s"),
+        "blanks": blanks,
         "strip": lambda: ts(T.strip[:, 3:515:4], T.iot[:, 0:128], T.pif[:, 0:1], None, AluOpType.is_equal, None,
                             [r("iot", 0, 128), r("pif")], [r("strip", 3, 515)]),
         "p15": lambda: ts(T.p15[:, 0:4], T.pi[:, 0:4], 15, None, AluOpType.bitwise_and, None, [r("pi")], [r("p15")]),
@@ -238,7 +281,16 @@ def rank_program(g, core, T, topo):
         "pa": lambda: ts(T.pa[:, 0:1], T.pi[:, 0:1], 3, None, AluOpType.bitwise_and, None, [r("pi")], [r("pa")]),
         "uoo": lambda: cp(T.uoo[:, 0:16], T.uoi[:, 0:16], [r("uoi")], [r("uoo")]),
         "pb2": lambda: ts(T.pb[:, 2:3], T.pa[:, 0:1], 64.0, 0.125, mult, add, [r("pa")], [r("pb", 2, 3)]),
-        "d4": lambda: picker("d4", "m4t", 64, 4, 0),
+        "d16": lambda: ts(T.d16[:, 0:256], T.s16t[:, 0:256], T.kap[:, 0:1], 256.0, AluOpType.is_gt, mult, [r("s16t"), r("kap")], [r("d16")]),
+        "da": lambda: ts(T.da[:, 0:16], T.s16t[:, 0:16], T.kap[:, 0:1], 2.0 ** -8, AluOpType.is_le, amax, [r("s16t"), r("kap")], [r("da")]),
+        "D16": factors,
+        "Pn": lambda: act(T.k1[:, 0:256], T.cm4[:, 0:256].indirect(T.nxo[:, 0:16]), F.Copy, [r("cm4"), r("nxo")], [r("k1")]),
+        "pn": lambda: tt(T.pk[:, 0:256], T.k1[:, 0:256], T.cm16[:, 0:256], add, [r("k1"), r("cm16")], [r("pk")]),
+        "u4": lambda: undo(0, 4),
+        "u16": lambda: undo(1, 1),
+        "zero": lambda: fill("zero", 0, 512, 0.0),
+        "z0": lambda: quant("hc", "hp", "zero", 0, 128),
+        "z1": lambda: quant("hc", "hp", "zero", 192, 128),
         "kv": lambda: act(T.kv[:, 0:4], T.kap[:, 0:4], F.Copy, [r("kap")], [r("kv")], bias=-63.0, scale=2.0),
         "ini": lambda: act(T.ini[:, 0:4], T.kap[:, 0:4], F.Copy, [r("kap")], [r("ini")], bias=17.0),
         "half": lambda: act(T.half[:, 0:PL], T.iot[:, 0:PL], F.Copy, [r("iot")], [r("half")], bias=0.5),
@@ -257,8 +309,8 @@ def rank_program(g, core, T, topo):
     }
     for b in range(4):
         steps["e%d" % b] = lambda b=b: const(b)
-    for w in START.split():
-        steps[w]()
+    setup.update(steps)
+    run(START, steps)
     need("y", [r("t0")], [])
     dma("y", "dwc", T.wq[:, 0:512].bitcast(dt.uint8), T.wc[:, 0:2048], [], [r("wq")])
     dma("y", "dws", T.wp[:, 0:512], T.ws[:, 0:512], [], [r("wp")])
@@ -267,14 +319,19 @@ def rank_program(g, core, T, topo):
         q, s, xq, xs = "q%d" % t, "s%d" % t, "xq%d" % t, "xs%d" % t
         to, frm = (rank + STEP[t]) % len(T.cores), (rank - STEP[t]) % len(T.cores)
         for h in range(2):
-            send("xa%d" % t, to, xq, 128 * h, q, 128 * h, 128)
-        send("xa%d" % t, to, xs, 0, s, 0, C)
-        arrival("xa%d" % t, frm, 3, [r(xq), r(xs)])
+            sem = "%sa%d" % ("xy"[h * HALF], t)
+            send(sem, to, xq, 128 * h, q, 128 * h, 128)
+            if HALF:
+                send(sem, to, xs, 128 * h, s, 128 * h, 128)
+                arrival(sem, frm, 2, [r(xq, 128 * h, 128 * h + 128), r(xs, 128 * h, 128 * h + 128)])
+        if not HALF:
+            send(sem, to, xs, 0, s, 0, C)
+            arrival(sem, frm, 3, [r(xq), r(xs)])
         if t == 0:
             whole("lt", 64, 65, [[0, 1]], -64)
-            whole("s16t", 0, 256, [[0, 16], [1, 16]])
-            for name, a, b in (("rr", 0, 128), ("rm", 0, 128), ("ht", 256, 512)):
-                whole(name, a, b, [[0, b - a]])
+            if VR:
+                whole("lt4", 0, 256, [[0, 4], [1, 64]])
+            zeros(("two", 0, 8), ("byr", 0, 64), ("rr", 0, 128))
 
         def lst(buf, k):
             a = 32 * t + LISTS[k][0]
@@ -284,10 +341,16 @@ def rank_program(g, core, T, topo):
             a = 32 * t + LISTS[k][0]
             send("%sa%d" % (k, t), to, "came", a, "mine", a, LISTS[k][1])
             arrival("%sa%d" % (k, t), frm, 1, [lst("came", k)[1]])
+            if (t, k) == (0, "o"):
+                zeros(("zt", 256, 512), ("ht", 256, 512), ("rm", 0, 128))
 
-        def unpack(cq, sq):
+        def unpack(buf, cq, sq):
             for b in range(4):
-                mm(b, "pf", 256, "eq", "esc", 128 * b, cq, sq, 0)
+                mm(b, buf, 256, "eq", "esc", 128 * b, cq, sq, 0)
+
+        def own(b):
+            n = min(C, OWN - C * b)
+            act(T.fo[:, C * b:C * b + n], T.pf[:, 512 * b:512 * b + n], F.Copy, [bank("pf", b)], [r("fo", C * b, C * b + n)])
         for h in range(2):
             for k in range(2):
                 mm(2 * h + k, "pw", 128, "uu", "us", 128 * k, q, s, 128 * h)
@@ -295,24 +358,40 @@ def rank_program(g, core, T, topo):
         def sign(h, k):
             n, a, e = ("sa", "sb")[k], 128 * h, 128 * h + 128
             i = T.pw[:, 1024 * h + 512 * k:1024 * h + 512 * k + 128]
-            if k == 0:
+            if k == 0 and h in VS:
                 ts(T[n][:, a:e], i, 0.0, 2.0, AluOpType.is_lt, mult, [bank("pw", 2 * h + k)], [r(n, a, e)])
             else:
                 act(T[n][:, a:e], i, F.Sign, [bank("pw", 2 * h + k)], [r(n, a, e)], bias=-1e-36, scale=-1.0)
 
         def key(h, k):
-            a, e = 128 * h, 128 * h + 128
+            a, e = (128 * h, 128 * h + 128) if h < 2 else (0, C)
             if k == 0:
                 tt(T.k1[:, a:e], T.sa[:, a:e], T.pk[:, a:e], add, [r("sa", a, e), r("pk", a, e)], [r("k1", a, e)])
             else:
                 tt(T.kr[:, a:e], T.k1[:, a:e], T.sb[:, a:e], mult, [r("k1", a, e), r("sb", a, e)], [r("kr", a, e)])
 
-        def plane(b, on):
-            copy(on, T.fh[:, PL * b:PL * b + C], T.pf[:, 512 * b:512 * b + C], [bank("pf", b)], [r("fh", PL * b, PL * b + C)])
+        def unpack_half(h, a=0, e=4):
+            for b in range(a, e):
+                mm(b, ("pf", "pw", "pw")[h], (128, 128, C)[h], "eq", "esc", 128 * b, xq, xs, 128 * (h % 2))
 
-        def mask(i):
-            ts(T["m%d" % i][:, 0:256], T.kr[:, 0:256], T.kv[:, i:i + 1], 2.0 ** -10, AluOpType.not_equal, amax,
-               [r("kr"), r("kv")], [r("m%d" % i, 0, 256)])
+        def plane(h, b, on):
+            a, buf, n = PL * b + 128 * (h % 2), ("pf", "pw", "pw")[h], (128, 128, C)[h]
+            copy(on, T.fh[:, a:a + n], T[buf][:, 512 * b:512 * b + n], [bank(buf, b)], [r("fh", a, a + n)])
+
+        def mask(i, h=2):
+            a, e = (128 * h, 128 * h + 128) if h < 2 else (0, C)
+            ts(T["m%d" % i][:, a:e], T.kr[:, a:e], T.kv[:, i:i + 1], 2.0 ** -10, AluOpType.not_equal, amax,
+               [r("kr", a, e), r("kv")], [r("m%d" % i, a, e)])
+
+        def side(i, h):
+            a = 128 * h
+            act(T.sg[:, C * (i - 2) + a:C * (i - 2) + a + 128], T.kr[:, a:a + 128], F.Sign, [r("kr", a, a + 128), r("kv")],
+                [r("sg", C * (i - 2) + a, C * (i - 2) + a + 128)], bias=T.kv[:, i:i + 1], scale=-1.0)
+
+        def size(i, h):
+            a = 128 * h
+            act(T["m%d" % i][:, a:a + 128], T.sg[:, C * (i - 2) + a:C * (i - 2) + a + 128], F.Abs,
+                [r("sg", C * (i - 2) + a, C * (i - 2) + a + 128)], [r("m%d" % i, a, a + 128)], bias=2.0 ** -10)
 
         def scan(i):
             a = 512 * i + 256
@@ -328,15 +407,18 @@ def rank_program(g, core, T, topo):
             a = 512 * i + 256
             act(T.junk[:, 256 * i:256 * i + 256], T["w%d" % i][:, 0:256], F.Copy, [r("w%d" % i)],
                 [r("junk", 256 * i, 256 * i + 256), r("ww", a, a + 1)], accum_out=T.ww[:, a:a + 1])
-        steps = {"g": sign, "k": key, "m": mask, "s": scan, "t": total, "F": lambda: unpack(xq, xs), "p": lambda b: plane(b, "s")}
-        for w in SEARCH.split():
-            steps[w[0]](*[int(ch) for ch in w[1:]])
+        steps = {"g": sign, "k": key, "m": mask, "s": scan, "t": total, "P": lambda: t > 0 or prekeys_next(),
+                 "F": unpack_half, "p": lambda h, b: plane(h, b, "s"), "own": lambda: unpack("pf", q, s), "o": own, "x": side, "y": size,
+                 "D": lambda: t > 0 or act(T.d64[:, 0:256], T.lt4[:, 0:256], F.Sign, [r("lt4")], [r("d64")])}
+        run(SEARCH, steps)
 
         vv, rv = T.ww[:, 256:2048:512], [r("ww", 512 * i + 256, 512 * i + 257) for i in range(4)]
         rg = [r("ww", 512 * i, 512 * i + 1) for i in range(4)]
         (f16, rf), (s16, rs), (o16, ro) = [lst("mine", k) for k in "fso"]
         (fin, rfin), (sin, rsin), (oin, roin) = [lst("came", k) for k in "fso"]
         row, rrow = T.half[:, 0:PL].indirect(f16), [r("half"), rf]
+        if TAIL:
+            row, rrow = T.half[:, 0:PL].indirect(T.fu[:, 0:4]), [r("half"), r("fu")]
         crow = "cr" if t < R - 1 else "cf"
 
         def rank_of_key(i):
@@ -361,14 +443,12 @@ def rank_program(g, core, T, topo):
                 ts(o, i, 0.5, None, mult, None, rd, wr)
 
         def ranks_row():
-            if t == 0:
-                picker("d16", "s16t", 256, 16, 1)
             ts(T.rr[:, 0:128:2], T.half[:, 0:64].indirect(T.r16[:, 0:4]), -0.5, None, add, None, [r("half"), r("r16")], [r("rr")])
 
-        def own():
-            unpack(q, s)
-            for b in range(2):
-                act(T.fo[:, C * b:C * b + C], T.pf[:, 512 * b:512 * b + C], F.Copy, [bank("pf", b)], [r("fo", C * b, C * b + C)])
+        def lower(i):
+            ts(T.lt4[:, 64 * i:64 * i + 64], T.fr[:, 0:64], T.ww[:, 512 * i + 256:512 * i + 257], None, AluOpType.is_lt, None,
+               [r("fr"), rv[i]], [r("lt4", 64 * i, 64 * i + 64)])
+
         steps = {
             "f16": lambda: cp(f16, vv, rv, [rf]),
             "two": lambda: ts(T.two[:, 0:8:2], T.sv8[:, 1:8:2], 0.25, 1024.0, AluOpType.is_lt, mult, [r("sv8")], [r("two")]),
@@ -377,24 +457,42 @@ def rank_program(g, core, T, topo):
             "G": lambda: ts(T.ww[:, 0:2048:512], vv, WHOLE, -WHOLE, add, add, rv, rg),
             "S": lambda: horner(T.sv8[:, 0:8], T.hor[:, 0:8], T.ww[:, 0:2048:256], 0.0, [r("hor")] + rv + rg, [r("sv8")]),
             "s16": lambda: ts(s16, T.sx8[:, 0:8:2], 0.0625, None, add, None, [r("sx8")], [rs]),
+            "n": lambda b: copy("s", T.gs[:, 64 * b:64 * b + 64], T.fh[:, PL * b:PL * b + PL].indirect(sin),
+                                [r("fh", PL * b, PL * b + PL), rsin], [r("gs", 64 * b, 64 * b + 64)]),
+            "M": lambda a, e: tt(T.zk[:, 64 * a:64 * e], T.gs[:, 64 * a:64 * e], T.g1[:, 64 * a:64 * e], add,
+                                 [r("gs", 64 * a, 64 * e), r("g1", 64 * a, 64 * e)], [r("zk", 64 * a, 64 * e)]),
+            "fu": lambda: cp(T.fu[:, 0:4], vv, rv, [r("fu")]),
+            "fz": lambda: ts(f16, vv, float(C), None, AluOpType.min, None, rv, [rf]),
+            "sz": lambda: ts(s16, T.sv8[:, 1:8:2], 1024.0, 0.0625, mult, add, [r("sv8")], [rs]),
+            "lu": lambda: ts(T.lu[:, 0:64], row, T.ww[:, 1280:1281], 2.0, AluOpType.is_lt, mult, rrow + [rv[2]], [r("lu", 0, 64)]),
+            "reu": lambda: op("v", lambda: V.tensor_reduce(T.acc[:, 2:3], T.lu[:, 0:65], AxisListType.X, add), [r("lu")], [r("acc", 2, 3)]),
+            "T": lambda b: copy("s", T.fh[:, PL * b + C + 16:PL * b + PL], T.fh[:, PL * b:PL * b + C + 16].indirect(fin),
+                                [r("fh", PL * b, PL * b + C + 16), rfin], [r("fh", PL * b + C + 16, PL * b + PL)]),
             "lt": lambda: ts(T.lt[:, 0:64], row, T.ww[:, 1792:1793], 2.0, AluOpType.is_lt, mult, rrow + [rv[3]], [r("lt", 0, 64)]),
             "red": lambda: op("v", lambda: V.tensor_reduce(T.acc[:, 3:4], T.lt[:, 0:65], AxisListType.X, add), [r("lt")], [r("acc", 3, 4)]),
             "r16": lambda: ts(T.r16[:, 0:4], T.acc[:, 0:4], 0.5, 32.0, mult, add, [r("acc")], [r("r16")]),
             "sc": lambda: cp(T.byr[:, 0:64].indirect(T.r16[:, 0:4]), T.iot[:, 0:64], [r("iot"), r("r16")], [r("byr")]),
-            "O": lambda: horner(T.byo[:, 0:64], T.d4[:, 0:64], T.byr[:, 0:64], 0.0, [r("d4"), r("byr")], [r("byo")]),
-            "o16": lambda: ts(o16, T.byo[:, 3:64:4], T.pb[:, 0:1], T.pb[:, 2:3], mult, add, [r("byo"), r("pb", 0, 3)], [ro]),
-            "F": lambda: unpack(xq, xs),
+            "O": lambda: horner(T.byo[:, 0:64], T.d16[:, 0:256:4], T.byr[:, 0:64], 0.0, [r("d16"), r("byr")], [r("byo")]),
+            "o16": lambda: ts(o16, T.byo[:, 3:64:4], T.pb[:, 0:1], T.pb[:, 2:3], mult, add, [r("byo"), r("pb", 0, 1), r("pb", 2, 3)], [ro]),
+            "F": unpack_half,
+            "p": lambda h, b: plane(h, b, "s"),
+            "P": lambda h, b: plane(h, b, "v"),
+            "own": lambda: unpack("pf", q, s),
             "rr": ranks_row,
             "kw": lambda: as_list("kr", "kw", 63.25),
+            "fr": lambda: cp(T.fr[:, 0:64], row, rrow, [r("fr")]),
+            "l": lower,
+            "A": lambda: horner(T.ac4[:, 0:256], T.d64[:, 0:256], T.lt4[:, 0:256], 0.0, [r("d64"), r("lt4")], [r("ac4")]),
+            "R16": lambda: cp(T.r16[:, 0:4], T.ac4[:, 63:256:64], [r("ac4")], [r("r16")]),
             "cr": lambda: cp(T[crow][:, 0:256], T.rr[:, 0:128].indirect(T.kw[:, 0:16]), [r("rr"), r("kw")], [r(crow)]),
             "Cr": lambda: act(T[crow][:, 0:256], T.rr[:, 0:128].indirect(T.kw[:, 0:16]), F.Copy, [r("rr"), r("kw")], [r(crow)]),
             "cw": lambda: as_list(crow, "cw", 0.125),
-            "own": own,
             "rm": lambda: cp(T.rm[:, 0:128:2], T.m4t[:, 0:64].indirect(T.r16[:, 0:4]), [r("m4t"), r("r16")], [r("rm")]),
             "cm4": lambda: copy("v", T.cm4[:, 0:256], T.rm[:, 0:128].indirect(T.kw[:, 0:16]), [r("rm"), r("kw")], [r("cm4")]),
             "Cm4": lambda: copy("s", T.cm4[:, 0:256], T.rm[:, 0:128].indirect(T.kw[:, 0:16]), [r("rm"), r("kw")], [r("cm4")]),
             "cm16": prekeys_own,
             "Cm16": lambda: prekeys_own("s"),
+            "Rr": lambda: act(T.rr[:, 0:128:2], T.half[:, 0:64].indirect(T.r16[:, 0:4]), F.Copy, [r("half"), r("r16")], [r("rr")], bias=-0.5),
             "Rm": lambda: copy("s", T.rm[:, 0:128:2], T.m4t[:, 0:64].indirect(T.r16[:, 0:4]), [r("m4t"), r("r16")], [r("rm")]),
             "pk": prekeys_next,
         }
@@ -406,11 +504,9 @@ def rank_program(g, core, T, topo):
             steps["v%d" % i] = lambda i=i: first(i, "v")
             steps["m%d" % i] = lambda i=i: mean(i)
             steps["z%d" % i] = lambda i=i: final(i)
-            steps["p%d" % i] = lambda i=i: plane(i, "s")
-            steps["P%d" % i] = lambda i=i: plane(i, "v")
-        for w in MEANS.split():
-            if t < R - 1 or w.lower() not in ("rm", "cm4", "cm16", "pk"):
-                steps[w]()
+            steps["o%d" % i] = lambda i=i: own(i)
+        skip = () if t < R - 1 else ("rm", "cm4", "cm16", "pk")
+        run(MEANS, steps, skip)
         quant("zc", "zp", "zt", 0, 128)
         for b in range(4):
             mm(b, "pw", 128, "wq", "wp", 128 * b, "zc", "zp", 0)
@@ -428,33 +524,36 @@ def rank_program(g, core, T, topo):
         if t == 0:
             need("y", [r("zc")], [])
             dma("y", "dv", T.vt[:], T.v[:], [], [r("vt")])
-            for a in (0, 192):
-                quant("hc", "hp", "zero", a, 128)
-        for w in AFTER.split():
-            if t < R - 1 or w.lower() not in ("rm", "cm4", "cm16", "pk"):
-                steps[w]()
+        run(AFTER, steps, skip)
         if t == R - 1:
             dma("y", "dol", T.ol[:], T.cf[0:128:16, 0:256], [r("cf")], [])
             quant("qv", "sv", "vt", 0, 128)
         new = "t%d" % (t + 1)
         for b in range(4):
             mm(min(b, 2), "pw", 128, "eq", "esc", 128 * b, "hc", "hp", land - 64 * (b == 3), b != 3, b != 2)
-        for b, n, on in ((0, 64, "v"), (1, 64, DH1), (2, 128, "s")):
+
+
+        def came_h(b, on):
+            n = 128 if b == 2 else 64
             copy(on, T.dh[:, 64 * b:64 * b + n], T.pw[:, 512 * b:512 * b + n], [bank("pw", b)], [r("dh", 64 * b, 64 * b + n)])
-        for h in range(2):
-            for b in (2, 3):
-                o = C * (b - 2) + 128 * h
-                act(T.g2[:, o:o + 128], T.dh[:, 64 * b:64 * b + 64].indirect(T.cw[:, 8 * h:8 * h + 8]), F.Copy,
-                    [r("dh", 64 * b, 64 * b + 64), r("cw")], [r("g2", o, o + 128)])
-        for b in (0, 1):
-            tt(T[new][:, b:1024:4], T.dh[:, 64 * b:64 * b + 64].indirect(T.cw[:, 0:16]), T.fo[:, C * b:C * b + C], add,
-               [r("dh", 64 * b, 64 * b + 64), r("cw"), r("fo", C * b, C * b + C)], [(new, C * b, C * b + C)])
-        for h in range(2):
-            for b in (2, 3):
-                o, p, w = C * (b - 2) + 128 * h, 512 * b + 128 * h, C * b + 128 * h
-                tt(T[new][:, 512 * h + b:512 * h + 512:4], T.g2[:, o:o + 128], T.pf[:, p:p + 128], add,
-                   [r("g2", o, o + 128), bank("pf", b)], [(new, w, w + 128)])
-            quant("q%d" % (t + 1), "s%d" % (t + 1), new, 128 * h, 128, 128 * h)
+
+        def picked(b, h):
+            o = C * (b - 2) + 128 * h
+            act(T.g2[:, o:o + 128], T.dh[:, 64 * b:64 * b + 64].indirect(T.cw[:, 8 * h:8 * h + 8]), F.Copy,
+                [r("dh", 64 * b, 64 * b + 64), r("cw")], [r("g2", o, o + 128)])
+
+        def both(b, a=0, e=2):
+            a, e = 128 * a, 128 * e
+            tt(T[new][:, 4 * a + b:4 * e:4], T.dh[:, 64 * b:64 * b + 64].indirect(T.cw[:, a // 16:e // 16]), T.fo[:, C * b + a:C * b + e], add,
+               [r("dh", 64 * b, 64 * b + 64), r("cw"), r("fo", C * b + a, C * b + e)], [(new, C * b + a, C * b + e)])
+
+        def added(b, h):
+            o, p, w = C * (b - 2) + 128 * h, 512 * b + 128 * h, C * b + 128 * h
+            tt(T[new][:, 512 * h + b:512 * h + 512:4], T.g2[:, o:o + 128], T.pf[:, p:p + 128], add,
+               [r("g2", o, o + 128), bank("pf", b)], [(new, w, w + 128)])
+        steps = {"d": lambda b: came_h(b, "v"), "D": lambda b: came_h(b, "s"), "G": picked, "b": both, "a": added,
+                 "q": lambda h: quant("q%d" % (t + 1), "s%d" % (t + 1), new, 128 * h, 128, 128 * h)}
+        run(EXPAND, steps)
 
     def store_scales(qu, k):
         dma(qu, "ds%d" % k, T.osc[4 * k:4 * k + 4, 0:256], T.s3[32 * k:32 * k + 4, 0:256], [r("s3")], [])

from concourse.mybir import dt, AluOpType, AxisListType, ActivationFunctionType

C, K, R = 256, 64, 3
STEP = [1, 2, 4]
PL = C + 16 + K
REV = (2, 3)
TRANS = True
UP = False
VS = (0, 1)
HALF = 0
VR = 0
TAIL = 0
DH1 = "v"
ZS = 8
VRELU = (2, 3)
CODES = "float8_e4m3fn_x4"
WHOLE = 1.5 * 2.0 ** 23
START = "blanks strip p15 e0 kap e1 kv ini uoo e2 coo cm4 qu e3 uu us lasts half hor x0 nxo cm16 pa pk x1"
SEARCH = "g01 g00 +d16 k00 g11 g10 k01 x30 x20 y30 k10 m00 k11 x31 y20 y31 m10 m01 m11 own s0 t0 m21 s1 t1 s2 s3 +da"
MEANS = "f16 G >f r0 r1 r2 lt S red two +pb2 X r16 s16 >s sc +u4 O o16 >o +u16 +zero F2 p20 p21 p22 p23 g0 g1 g2 g3 Rr kw m0 m1 m2 m3 z0 z1"
AFTER = "+z0 +z1 Rm cr Cm4 Cm16 o0 o1 cw pk"
EXPAND = "d0 d1 D2 G20 G30 G21 G31 b0 b1 a20 a30 a21 q0 a31 q1"
LOADS = "yu yx0 yx1 sc sn"
OWN = 512
PICK = "b"

SCRATCH = {}
for _n, _w, _d in (
        ("ones", 784, "b"), ("strip", 516, "b"), ("zero", 512, "b"), ("eq", 512, "c"), ("esc", 512, "p"), ("ut", 512, "b"), ("qu", 128, "c"),
        ("su", 128, "p"), ("uu", 256, "c"), ("us", 256, "p"), ("vt", 512, "b"), ("qv", 128, "c"), ("sv", 128, "p"), ("wq", 512, "c"), ("wp", 512, "p"),
        ("nxi", 16, "i"), ("coi", 16, "i"), ("nxo", 16, "u"), ("coo", 16, "u"), ("uoi", 16, "i"), ("uoo", 16, "u"), ("iot", PL, "f"), ("pif", 1, "f"),
        ("half", PL, "f"), ("m4t", 64, "b"), ("pi", 4, "i"), ("p15", 4, "i"), ("si", 4, "i"), ("kap", 4, "f"), ("kv", 4, "f"), ("ini", 4, "f"),
        ("pa", 4, "i"), ("pb", 4, "f"), ("da", 16, "b"), ("fr", 64, "f"), ("lt4", 256, "b"), ("d64", 256, "b"), ("ac4", 256, "b"), ("d16", 256, "b"), ("s16t", 256, "b"),
        ("fh", 4 * PL, "b"), ("sa", 256, "b"), ("sb", 256, "b"), ("hor", 8, "f"), ("sv8", 8, "f"), ("two", 8, "f"), ("sx8", 8, "f"),
        ("k1", 256, "b"), ("pk", 256, "b"), ("cm4", 256, "b"), ("cm16", 256, "b"), ("kr", 256, "b"), ("cr", 256, "b"), ("pick", 256, PICK),
        ("kw", 16, "u"), ("cw", 16, "u"), ("junk", 768, "b"), ("jun2", 256, "f"),
        ("ww", 2048, "f"), ("acc", 4, "f"), ("lt", 65, "b"), ("lu", 65, "b"), ("fu", 4, "u"), ("gs", 256, "b"), ("sg", 512, "b"), ("g1", 256, "b"), ("r16", 4, "u"), ("mine", 32 * R, "u"), ("came", 32 * R, "u"), ("fo", 1024, "b"),
        ("rr", 128, "b"), ("rm", 128, "b"), ("byr", 64, "b"), ("byo", 64, "f"), ("zk", 256, "b"),
        ("zt", 512, "b"), ("ht", 512, "b"), ("dh", 256, "b"), ("g2", 512, "b"), ("cf", 256, "f"),
        ("yo", 256, "f"), ("w0", 256, "b"), ("w1", 256, "b"), ("w2", 256, "b"),
        ("zc", 128, "c"), ("zp", 128, "p"), ("hc", 320, "c"), ("hp", 320, "p")):
    SCRATCH[_n] = ("sbuf", [128, _w], {"b": "bfloat16", "c": CODES, "p": "uint8", "i": "int32", "u": "uint16", "f": "float32"}[_d])
for _n in ("pf", "pw"):
    SCRATCH[_n] = ("psum", [128, 2048], "float32")
for _i in range(4):
    SCRATCH["m%d" % _i] = ("sbuf", [128, 256], "bfloat16")
    SCRATCH["t%d" % _i] = ("sbuf", [128, 1024], "bfloat16")
    SCRATCH["q%d" % _i] = ("sbuf", [128, 256], CODES)
    SCRATCH["s%d" % _i] = ("sbuf", [128, 256], "uint8")
for _i in range(R):
    for _n, _w in (("h", 128), ("x", 256)):
        SCRATCH["%sq%d" % (_n, _i)] = ("sbuf", [128, _w], CODES)
        SCRATCH["%ss%d" % (_n, _i)] = ("sbuf", [128, _w], "uint8")
LISTS = {"f": (0, 4), "s": (8, 4), "o": (16, 16)}

DMAS = ["dx0", "dx1", "du", "dv", "dwc", "dws", "dn", "dc", "dol", "doc0", "dy0", "doc1", "ds0", "ds1", "ds2", "ds3", "dy1"]
SEMAPHORES = ["cv", "cs", "ct", "cg", "left"] + ["%sa%d" % (_n, _i) for _n in "xyfsoh" for _i in range(R)] + DMAS


def rank_program(g, core, T, topo):
    rank = T.rank_of(core)
    if rank is None:
        return
    add, mult, amax = AluOpType.add, AluOpType.mult, AluOpType.max
    F = ActivationFunctionType
    eng = {"v": g.vector, "s": g.scalar, "t": g.tensor, "g": g, "y": g.sync}
    count = {"cv": 0, "cs": 0, "ct": 0, "cg": 0, "left": 0}
    known = {q: {} for q in eng}
    wrote, read = {}, {}
    behind = {}

    def over(book, reg):
        return [e for e in book.get(reg[0], []) if e[0] < reg[2] and reg[1] < e[1]]

    def need(q, reads, writes):
        want = {}
        for reg in reads:
            for e in over(wrote, reg):
                want[e[3]] = max(want.get(e[3], 0), e[4])
            if reg[0] in ("pf", "pw"):
                for e in over(read, reg):
                    if e[2] != q:
                        want[e[3]] = max(want.get(e[3], 0), e[4])
        for reg in writes:
            for e in over(wrote, reg):
                want[e[3]] = max(want.get(e[3], 0), e[4])
            for e in over(read, reg):
                if e[2] != q:
                    want[e[3]] = max(want.get(e[3], 0), e[4])
        for s in want:
            if any(behind.get((o, want[o]), {}).get(s, 0) >= want[s] for o in want if o != s):
                want[s] = 0
        for s in sorted(want):
            if known[q].get(s, 0) < want[s]:
                if UP and s == "c" + q:
                    want[s] = max(want[s], count[s] - 1)
                eng[q].wait_ge(T.sem[s], want[s])
                known[q][s] = want[s]
                for o, n in behind.get((s, want[s]), {}).items():
                    known[q][o] = max(known[q].get(o, 0), n)

    def note(q, reads, writes, s, n):
        if TRANS and q in known:
            behind[(s, n)] = dict(known[q])
        for reg in writes:
            for book in (wrote, read):
                book[reg[0]] = [e for e in book.get(reg[0], []) if not (reg[1] <= e[0] and e[1] <= reg[2])]
            wrote[reg[0]].append((reg[1], reg[2], q, s, n))
        for reg in reads:
            book = [e for e in read.get(reg[0], []) if not (e[2] == q and reg[1] <= e[0] and e[1] <= reg[2])]
            book.append((reg[1], reg[2], q, s, n))
            read[reg[0]] = book

    def op(q, call, reads, writes, adds=False):
        need(q, reads, [] if adds else writes)
        s = "c" + q
        count[s] += 1
        call().then_inc(T.sem[s], 1)
        note(q, reads, writes, s, count[s])

    def ahead(w):
        q, s = w[1], "c" + w[2]
        if known[q].get(s, 0) < count[s]:
            eng[q].wait_ge(T.sem[s], count[s])
            known[q][s] = count[s]
            for o, n in behind.get((s, count[s]), {}).items():
                known[q][o] = max(known[q].get(o, 0), n)

    setup = {}

    def run(order, steps, skip=()):
        for w in order.split():
            if w[0] == "^":
                ahead(w)
            elif w[0] == "+":
                if w[1:] in setup:
                    setup.pop(w[1:])()
            elif w.lower() in skip:
                continue
            elif w in steps:
                steps[w]()
            else:
                steps[w[0]](*[int(ch) for ch in w[1:]])

    def dma(q, s, out, in_, reads, writes):
        need(q, reads, writes)
        eng[q].dma_start(out, in_).then_inc(T.sem[s], 16)
        note(q, reads, writes, s, 16)

    V, S, PE = g.vector, g.scalar, g.tensor

    def r(name, a=0, b=None):
        return (name, a, T[name].shape[1] if b is None else b)

    def quant(qb, sb_, tile, a, n, c0=0):
        if tile == "t0":
            src = [(tile, 4 * c0, 4 * (c0 + n))]
        elif tile in ("t1", "t2", "t3"):
            src = [(tile, C * b + c0, C * b + c0 + n) for b in range(4)]
        else:
            src = [r(tile)]
        op("v", lambda: V.quantize_mx(T[qb][:, a:a + n], T[sb_][:, a:a + n], T[tile][:, 4 * c0:4 * (c0 + n)]),
           src, [r(qb, a, a + n), r(sb_, a, a + n)])

    def fill(name, a, b, val, step=1):
        op("v", lambda: V.memset(T[name][:, a:b:step], val), [], [r(name, a, b)])

    def whole(name, a, b, pattern, base=0, per=0):
        op("g", lambda: g.iota(T[name][:, a:b], pattern, base, per, allow_small_or_imprecise_dtypes=True), [], [r(name, a, b)])

    def ts(out, in0, s1, s2, op0, op1, reads, writes):
        if s2 is None:
            op("v", lambda: V.tensor_scalar(out, in0, s1, None, op0), reads, writes)
        else:
            op("v", lambda: V.tensor_scalar(out, in0, s1, s2, op0, op1), reads, writes)

    def tt(out, a, b, o, reads, writes):
        op("v", lambda: V.tensor_tensor(out, a, b, o), reads, writes)

    def cp(out, a, reads, writes):
        op("v", lambda: V.tensor_copy(out, a), reads, writes)

    def horner(out, d0, d1, first, reads, writes):
        op("v", lambda: V.tensor_tensor_scan(out, d0, d1, first, mult, add), reads, writes)

    def act(out, a, f, reads, writes, **kw):
        op("s", lambda: S.activation(out, a, f, **kw), reads, writes)

    def copy(on, out, a, reads, writes):
        if on == "s":
            act(out, a, F.Copy, reads, writes)
        else:
            cp(out, a, reads, writes)

    def bank(buf, b):
        return (buf, 512 * b, 512 * b + 512)

    def mm(b, buf, n, lq, ls, la, rq, rs, ra, start=True, stop=True):
        op("t", lambda: PE.matmul_mx(T[buf][:, 512 * b:512 * b + n], T[lq][:, la:la + 128], T[ls][:, la:la + 128],
                                     T[rq][:, ra:ra + n], T[rs][:, ra:ra + n], start, stop),
           [r(lq, la, la + 128), r(ls, la, la + 128), r(rq, ra, ra + n), r(rs, ra, ra + n)], [bank(buf, b)], not start)

    def send(sem, peer, there, a, here, c, n):
        need("g", [r(here, c, c + n)], [])
        dst = T.cores[peer]
        rid, pid, _se = topo.addr(dst)
        o, i = T[there][:, a:a + n], T[here][:, c:c + n]
        if SCRATCH[here][2] == CODES:
            o, i = o.bitcast(dt.uint8), i.bitcast(dt.uint8)
        g.remote_dma(o, i, T.sem[sem], T.sem.left, pid, rid, topo.mask(core, dst))
        count["left"] += len(topo.engines(core, dst))

    def arrival(sem, peer, calls, regions):
        note("r", [], regions, sem, calls * len(topo.engines(T.cores[peer], core)))

    def undo(col, step):
        op("v", lambda: V.tensor_reduce(T.pb[:, col:col + 1], T.da[:, 0:16:step], AxisListType.X, mult), [r("da")], [r("pb", col, col + 1)])

    def as_list(row, dest, base):
        horner(T.pick[:, 0:256], T.d16[:, 0:256], T[row][:, 0:256], 0.0, [r("d16"), r(row)], [r("pick")])
        ts(T[dest][:, 0:16], T.pick[:, 15:256:16], T.pb[:, 1:2], base, mult, add, [r("pick"), r("pb", 1, 2)], [r(dest)])

    def prekeys_own(on="v"):
        for a, e in ((0, 128), (128, C)) if len(VS) == 1 else ((0, C),):
            bias = 1.0 if a // 128 in VS else 2.0
            if on == "s":
                act(T.cm16[:, a:e], T.cm4[:, a:e], F.Copy, [r("cm4")], [r("cm16", a, e)], scale=4.0, bias=bias)
            else:
                ts(T.cm16[:, a:e], T.cm4[:, a:e], 4.0, bias, mult, add, [r("cm4")], [r("cm16", a, e)])

    def prekeys_next():
        tt(T.pk[:, 0:256], T.cm4[:, 0:256].indirect(T.nxo[:, 0:16]), T.cm16[:, 0:256], add, [r("cm4"), r("nxo"), r("cm16")], [r("pk")])

    loads = {"u": (T.ut[:], T.u[:], r("ut")), "c": (T.coi[:], T.co[:], r("coi")), "n": (T.nxi[:], T.nx[:], r("nxi"))}
    for h in range(2):
        loads["x%d" % h] = (T.t0[:, 512 * h:512 * h + 512], T.x[:, 512 * h:512 * h + 512], r("t0", 512 * h, 512 * h + 512))
    for w in LOADS.split():
        dma(w[0], "d" + w[1:], loads[w[1:]][0], loads[w[1:]][1], [], [loads[w[1:]][2]])
    fill("strip", 0, 516, 0.0)
    whole("pif", 0, 1, [[0, 1]], 0, 1)
    whole("iot", 0, 128, [[1, 128]])
    whole("pi", 0, 4, [[0, 4]], 0, 1)
    whole("si", 0, 4, [[16, 4]])
    whole("uoi", 0, 16, [[1, 2], [16, 8]])
    whole("m4t", 0, 64, [[0, 16], [4, 4]])
    fill("ones", 16, 16 + 256 * REV[0], 1.0)
    whole("ones", 15, 16, [[0, 1]])
    whole("iot", 128, PL, [[1, PL - 128]], 128)
    whole("sx8", 0, 8, [[0, 4], [-1023, 2]])
    whole("s16t", 0, 256, [[0, 16], [1, 16]])

    def blanks():
        for b in range(4):
            act(T.fh[:, PL * b + C:PL * b + PL], T.iot[:, 0:PL - C], F.Copy, [r("iot", 0, PL - C)], [r("fh", PL * b + C, PL * b + PL)], scale=0.0)

    def zeros(*runs):
        for name, a, b in runs:
            whole(name, a, b, [[0, b - a]])

    def const(b):
        op("v", lambda: V.quantize_mx(T.eq[:, 128 * b:128 * b + 128], T.esc[:, 128 * b:128 * b + 128], T.strip[:, 3 - b:515 - b]),
           [r("strip")], [r("eq", 128 * b, 128 * b + 128), r("esc", 128 * b, 128 * b + 128)])

    def factors():
        act(T.pb[:, 3:4], T.kap[:, 0:1], F.Copy, [r("kap")], [r("pb", 3, 4)], scale=-1.0, bias=-0.5)
        act(T.pick[:, 0:256], T.s16t[:, 0:256], F.Sign, [r("s16t"), r("pb", 3, 4)], [r("pick")], bias=T.pb[:, 3:4])
        act(T.da[:, 0:16], T.pick[:, 0:16], F.Copy, [r("pick")], [r("da")], scale=-255.0 / 512.0, bias=257.0 / 512.0)
        act(T.d16[:, 0:256], T.pick[:, 0:256], F.Relu, [r("pick")], [r("d16")], scale=256.0)

    def lasts():
        for i in range(REV[0]):
            act(T.ones[:, 271 + 256 * i:272 + 256 * i], T.ini[:, i:i + 1], F.Copy, [r("ini")], [r("ones", 271 + 256 * i, 272 + 256 * i)])
    steps = {
        "hor": lambda: act(T.hor[:, 0:8], T.sx8[:, 0:8], F.Copy, [r("sx8")], [r("hor")], scale=2.0 ** -10),
        "Cm16": lambda: prekeys_own("s"),
        "blanks": blanks,
        "strip": lambda: ts(T.strip[:, 3:515:4], T.iot[:, 0:128], T.pif[:, 0:1], None, AluOpType.is_equal, None,
                            [r("iot", 0, 128), r("pif")], [r("strip", 3, 515)]),
        "p15": lambda: ts(T.p15[:, 0:4], T.pi[:, 0:4], 15, None, AluOpType.bitwise_and, None, [r("pi")], [r("p15")]),
        "kap": lambda: tt(T.kap[:, 0:4], T.p15[:, 0:4], T.si[:, 0:4], add, [r("p15"), r("si")], [r("kap")]),
        "pa": lambda: ts(T.pa[:, 0:1], T.pi[:, 0:1], 3, None, AluOpType.bitwise_and, None, [r("pi")], [r("pa")]),
        "uoo": lambda: cp(T.uoo[:, 0:16], T.uoi[:, 0:16], [r("uoi")], [r("uoo")]),
        "pb2": lambda: ts(T.pb[:, 2:3], T.pa[:, 0:1], 64.0, 0.125, mult, add, [r("pa")], [r("pb", 2, 3)]),
        "d16": lambda: ts(T.d16[:, 0:256], T.s16t[:, 0:256], T.kap[:, 0:1], 256.0, AluOpType.is_gt, mult, [r("s16t"), r("kap")], [r("d16")]),
        "da": lambda: ts(T.da[:, 0:16], T.s16t[:, 0:16], T.kap[:, 0:1], 2.0 ** -8, AluOpType.is_le, amax, [r("s16t"), r("kap")], [r("da")]),
        "D16": factors,
        "Pn": lambda: act(T.k1[:, 0:256], T.cm4[:, 0:256].indirect(T.nxo[:, 0:16]), F.Copy, [r("cm4"), r("nxo")], [r("k1")]),
        "pn": lambda: tt(T.pk[:, 0:256], T.k1[:, 0:256], T.cm16[:, 0:256], add, [r("k1"), r("cm16")], [r("pk")]),
        "u4": lambda: undo(0, 4),
        "u16": lambda: undo(1, 1),
        "zero": lambda: fill("zero", 0, 512, 0.0),
        "z0": lambda: quant("hc", "hp", "zero", 0, 128),
        "z1": lambda: quant("hc", "hp", "zero", 192, 128),
        "kv": lambda: act(T.kv[:, 0:4], T.kap[:, 0:4], F.Copy, [r("kap")], [r("kv")], bias=-63.0, scale=2.0),
        "ini": lambda: act(T.ini[:, 0:4], T.kap[:, 0:4], F.Copy, [r("kap")], [r("ini")], bias=17.0),
        "half": lambda: act(T.half[:, 0:PL], T.iot[:, 0:PL], F.Copy, [r("iot")], [r("half")], bias=0.5),
        "coo": lambda: cp(T.coo[:, 0:16], T.coi[:, 0:16], [r("coi")], [r("coo")]),
        "qu": lambda: quant("qu", "su", "ut", 0, 128),
        "cm4": lambda: act(T.cm4[:, 0:256], T.m4t[:, 0:64].indirect(T.coo[:, 0:16]), F.Copy, [r("m4t"), r("coo")], [r("cm4")]),
        "uu": lambda: cp(T.uu[:, 0:256].bitcast(dt.uint32), T.qu[:, 0:128].bitcast(dt.uint32).indirect(T.uoo[:, 0:16]),
                         [r("qu"), r("uoo")], [r("uu")]),
        "us": lambda: act(T.us[:, 0:256], T.su[:, 0:128].indirect(T.uoo[:, 0:16]), F.Copy, [r("su"), r("uoo")], [r("us")]),
        "cm16": prekeys_own,
        "lasts": lasts,
        "x0": lambda: quant("q0", "s0", "t0", 0, 128, 0),
        "x1": lambda: quant("q0", "s0", "t0", 128, 128, 128),
        "nxo": lambda: cp(T.nxo[:, 0:16], T.nxi[:, 0:16], [r("nxi")], [r("nxo")]),
        "pk": prekeys_next,
    }
    for b in range(4):
        steps["e%d" % b] = lambda b=b: const(b)
    setup.update(steps)
    run(START, steps)
    need("y", [r("t0")], [])
    dma("y", "dwc", T.wq[:, 0:512].bitcast(dt.uint8), T.wc[:, 0:2048], [], [r("wq")])
    dma("y", "dws", T.wp[:, 0:512], T.ws[:, 0:512], [], [r("wp")])

    for t in range(R):
        q, s, xq, xs = "q%d" % t, "s%d" % t, "xq%d" % t, "xs%d" % t
        to, frm = (rank + STEP[t]) % len(T.cores), (rank - STEP[t]) % len(T.cores)
        for h in range(2):
            sem = "%sa%d" % ("xy"[h * HALF], t)
            send(sem, to, xq, 128 * h, q, 128 * h, 128)
            if HALF:
                send(sem, to, xs, 128 * h, s, 128 * h, 128)
                arrival(sem, frm, 2, [r(xq, 128 * h, 128 * h + 128), r(xs, 128 * h, 128 * h + 128)])
        if not HALF:
            send(sem, to, xs, 0, s, 0, C)
            arrival(sem, frm, 3, [r(xq), r(xs)])
        if t == 0:
            whole("lt", 64, 65, [[0, 1]], -64)
            if VR:
                whole("lt4", 0, 256, [[0, 4], [1, 64]])
            zeros(("two", 0, 8), ("byr", 0, 64), ("rr", 0, 128))

        def lst(buf, k):
            a = 32 * t + LISTS[k][0]
            return T[buf][:, a:a + LISTS[k][1]], r(buf, a, a + LISTS[k][1])

        def send_list(k):
            a = 32 * t + LISTS[k][0]
            send("%sa%d" % (k, t), to, "came", a, "mine", a, LISTS[k][1])
            arrival("%sa%d" % (k, t), frm, 1, [lst("came", k)[1]])
            if (t, k) == (0, "o"):
                zeros(("zt", 256, 512), ("ht", 256, 512), ("rm", 0, 128))

        def unpack(buf, cq, sq):
            for b in range(4):
                mm(b, buf, 256, "eq", "esc", 128 * b, cq, sq, 0)

        def own(b):
            n = min(C, OWN - C * b)
            act(T.fo[:, C * b:C * b + n], T.pf[:, 512 * b:512 * b + n], F.Copy, [bank("pf", b)], [r("fo", C * b, C * b + n)])
        for h in range(2):
            for k in range(2):
                mm(2 * h + k, "pw", 128, "uu", "us", 128 * k, q, s, 128 * h)

        def sign(h, k):
            n, a, e = ("sa", "sb")[k], 128 * h, 128 * h + 128
            i = T.pw[:, 1024 * h + 512 * k:1024 * h + 512 * k + 128]
            if k == 0 and h in VS:
                ts(T[n][:, a:e], i, 0.0, 2.0, AluOpType.is_lt, mult, [bank("pw", 2 * h + k)], [r(n, a, e)])
            else:
                act(T[n][:, a:e], i, F.Sign, [bank("pw", 2 * h + k)], [r(n, a, e)], bias=-1e-36, scale=-1.0)

        def key(h, k):
            a, e = (128 * h, 128 * h + 128) if h < 2 else (0, C)
            if k == 0:
                tt(T.k1[:, a:e], T.sa[:, a:e], T.pk[:, a:e], add, [r("sa", a, e), r("pk", a, e)], [r("k1", a, e)])
            else:
                tt(T.kr[:, a:e], T.k1[:, a:e], T.sb[:, a:e], mult, [r("k1", a, e), r("sb", a, e)], [r("kr", a, e)])

        def unpack_half(h, a=0, e=4):
            for b in range(a, e):
                mm(b, ("pf", "pw", "pw")[h], (128, 128, C)[h], "eq", "esc", 128 * b, xq, xs, 128 * (h % 2))

        def plane(h, b, on):
            a, buf, n = PL * b + 128 * (h % 2), ("pf", "pw", "pw")[h], (128, 128, C)[h]
            copy(on, T.fh[:, a:a + n], T[buf][:, 512 * b:512 * b + n], [bank(buf, b)], [r("fh", a, a + n)])

        def mask(i, h=2):
            a, e = (128 * h, 128 * h + 128) if h < 2 else (0, C)
            ts(T["m%d" % i][:, a:e], T.kr[:, a:e], T.kv[:, i:i + 1], 2.0 ** -10, AluOpType.not_equal, amax,
               [r("kr", a, e), r("kv")], [r("m%d" % i, a, e)])

        def side(i, h):
            a = 128 * h
            act(T.sg[:, C * (i - 2) + a:C * (i - 2) + a + 128], T.kr[:, a:a + 128], F.Sign, [r("kr", a, a + 128), r("kv")],
                [r("sg", C * (i - 2) + a, C * (i - 2) + a + 128)], bias=T.kv[:, i:i + 1], scale=-1.0)

        def size(i, h):
            a = 128 * h
            act(T["m%d" % i][:, a:a + 128], T.sg[:, C * (i - 2) + a:C * (i - 2) + a + 128], F.Abs,
                [r("sg", C * (i - 2) + a, C * (i - 2) + a + 128)], [r("m%d" % i, a, a + 128)], bias=2.0 ** -10)

        def scan(i):
            a = 512 * i + 256
            if i in REV:
                horner(T.ww[:, a + 255:a - 1:-1], T["m%d" % i][:, 255::-1], T.ones[:, 270:14:-1], T.ini[:, i:i + 1],
                       [r("m%d" % i), r("ones", 15, 271), r("ini")], [r("ww", a, a + 256)])
            else:
                op("v", lambda: V.tensor_tensor_scan(T["w%d" % i][:, 0:256], T["m%d" % i][:, 0:256], T.ones[:, 16 + 256 * i:272 + 256 * i],
                                                     1.0, mult, mult),
                   [r("m%d" % i), r("ones", 16 + 256 * i, 272 + 256 * i)], [r("w%d" % i)])

        def total(i):
            a = 512 * i + 256
            act(T.junk[:, 256 * i:256 * i + 256], T["w%d" % i][:, 0:256], F.Copy, [r("w%d" % i)],
                [r("junk", 256 * i, 256 * i + 256), r("ww", a, a + 1)], accum_out=T.ww[:, a:a + 1])
        steps = {"g": sign, "k": key, "m": mask, "s": scan, "t": total, "P": lambda: t > 0 or prekeys_next(),
                 "F": unpack_half, "p": lambda h, b: plane(h, b, "s"), "own": lambda: unpack("pf", q, s), "o": own, "x": side, "y": size,
                 "D": lambda: t > 0 or act(T.d64[:, 0:256], T.lt4[:, 0:256], F.Sign, [r("lt4")], [r("d64")])}
        run(SEARCH, steps)

        vv, rv = T.ww[:, 256:2048:512], [r("ww", 512 * i + 256, 512 * i + 257) for i in range(4)]
        rg = [r("ww", 512 * i, 512 * i + 1) for i in range(4)]
        (f16, rf), (s16, rs), (o16, ro) = [lst("mine", k) for k in "fso"]
        (fin, rfin), (sin, rsin), (oin, roin) = [lst("came", k) for k in "fso"]
        row, rrow = T.half[:, 0:PL].indirect(f16), [r("half"), rf]
        if TAIL:
            row, rrow = T.half[:, 0:PL].indirect(T.fu[:, 0:4]), [r("half"), r("fu")]
        crow = "cr" if t < R - 1 else "cf"

        def rank_of_key(i):
            act(T.jun2[:, 64 * i:64 * i + 64], row, F.Sign, rrow + [rv[i]], [r("jun2", 64 * i, 64 * i + 64), r("acc", i, i + 1)],
                bias=T.ww[:, 512 * i + 256:512 * i + 257], scale=-1.0, accum_out=T.acc[:, i:i + 1])

        def first(b, on):
            copy(on, T.g1[:, 64 * b:64 * b + 64], T.fh[:, PL * b:PL * b + PL].indirect(fin),
                 [r("fh", PL * b, PL * b + PL), rfin], [r("g1", 64 * b, 64 * b + 64)])

        def mean(b):
            tt(T.zk[:, 64 * b:64 * b + 64], T.fh[:, PL * b:PL * b + PL].indirect(sin), T.g1[:, 64 * b:64 * b + 64], add,
               [r("fh", PL * b, PL * b + PL), rsin, r("g1", 64 * b, 64 * b + 64)], [r("zk", 64 * b, 64 * b + 64)])

        def final(h):
            a, e = ((0, ZS), (ZS, 16))[h]
            o, i, rd, wr = T.zt[:, 16 * a:16 * e], T.zk[:, 0:256].indirect(T.came[:, roin[1] + a:roin[1] + e]), \
                [r("zk"), roin], [("zt", 16 * a, 16 * e)]
            if h == 0:
                act(o, i, F.Copy, rd, wr, scale=0.5)
            else:
                ts(o, i, 0.5, None, mult, None, rd, wr)

        def ranks_row():
            ts(T.rr[:, 0:128:2], T.half[:, 0:64].indirect(T.r16[:, 0:4]), -0.5, None, add, None, [r("half"), r("r16")], [r("rr")])

        def lower(i):
            ts(T.lt4[:, 64 * i:64 * i + 64], T.fr[:, 0:64], T.ww[:, 512 * i + 256:512 * i + 257], None, AluOpType.is_lt, None,
               [r("fr"), rv[i]], [r("lt4", 64 * i, 64 * i + 64)])

        steps = {
            "f16": lambda: cp(f16, vv, rv, [rf]),
            "two": lambda: ts(T.two[:, 0:8:2], T.sv8[:, 1:8:2], 0.25, 1024.0, AluOpType.is_lt, mult, [r("sv8")], [r("two")]),
            "X": lambda: op("v", lambda: V.tensor_tensor_scan(T.sx8[:, 7::-1], T.two[:, 7::-1], T.sv8[:, 7::-1], 0.0, mult, amax),
                            [r("two"), r("sv8")], [r("sx8")]),
            "G": lambda: ts(T.ww[:, 0:2048:512], vv, WHOLE, -WHOLE, add, add, rv, rg),
            "S": lambda: horner(T.sv8[:, 0:8], T.hor[:, 0:8], T.ww[:, 0:2048:256], 0.0, [r("hor")] + rv + rg, [r("sv8")]),
            "s16": lambda: ts(s16, T.sx8[:, 0:8:2], 0.0625, None, add, None, [r("sx8")], [rs]),
            "n": lambda b: copy("s", T.gs[:, 64 * b:64 * b + 64], T.fh[:, PL * b:PL * b + PL].indirect(sin),
                                [r("fh", PL * b, PL * b + PL), rsin], [r("gs", 64 * b, 64 * b + 64)]),
            "M": lambda a, e: tt(T.zk[:, 64 * a:64 * e], T.gs[:, 64 * a:64 * e], T.g1[:, 64 * a:64 * e], add,
                                 [r("gs", 64 * a, 64 * e), r("g1", 64 * a, 64 * e)], [r("zk", 64 * a, 64 * e)]),
            "fu": lambda: cp(T.fu[:, 0:4], vv, rv, [r("fu")]),
            "fz": lambda: ts(f16, vv, float(C), None, AluOpType.min, None, rv, [rf]),
            "sz": lambda: ts(s16, T.sv8[:, 1:8:2], 1024.0, 0.0625, mult, add, [r("sv8")], [rs]),
            "lu": lambda: ts(T.lu[:, 0:64], row, T.ww[:, 1280:1281], 2.0, AluOpType.is_lt, mult, rrow + [rv[2]], [r("lu", 0, 64)]),
            "reu": lambda: op("v", lambda: V.tensor_reduce(T.acc[:, 2:3], T.lu[:, 0:65], AxisListType.X, add), [r("lu")], [r("acc", 2, 3)]),
            "T": lambda b: copy("s", T.fh[:, PL * b + C + 16:PL * b + PL], T.fh[:, PL * b:PL * b + C + 16].indirect(fin),
                                [r("fh", PL * b, PL * b + C + 16), rfin], [r("fh", PL * b + C + 16, PL * b + PL)]),
            "lt": lambda: ts(T.lt[:, 0:64], row, T.ww[:, 1792:1793], 2.0, AluOpType.is_lt, mult, rrow + [rv[3]], [r("lt", 0, 64)]),
            "red": lambda: op("v", lambda: V.tensor_reduce(T.acc[:, 3:4], T.lt[:, 0:65], AxisListType.X, add), [r("lt")], [r("acc", 3, 4)]),
            "r16": lambda: ts(T.r16[:, 0:4], T.acc[:, 0:4], 0.5, 32.0, mult, add, [r("acc")], [r("r16")]),
            "sc": lambda: cp(T.byr[:, 0:64].indirect(T.r16[:, 0:4]), T.iot[:, 0:64], [r("iot"), r("r16")], [r("byr")]),
            "O": lambda: horner(T.byo[:, 0:64], T.d16[:, 0:256:4], T.byr[:, 0:64], 0.0, [r("d16"), r("byr")], [r("byo")]),
            "o16": lambda: ts(o16, T.byo[:, 3:64:4], T.pb[:, 0:1], T.pb[:, 2:3], mult, add, [r("byo"), r("pb", 0, 1), r("pb", 2, 3)], [ro]),
            "F": unpack_half,
            "p": lambda h, b: plane(h, b, "s"),
            "P": lambda h, b: plane(h, b, "v"),
            "own": lambda: unpack("pf", q, s),
            "rr": ranks_row,
            "kw": lambda: as_list("kr", "kw", 63.25),
            "fr": lambda: cp(T.fr[:, 0:64], row, rrow, [r("fr")]),
            "l": lower,
            "A": lambda: horner(T.ac4[:, 0:256], T.d64[:, 0:256], T.lt4[:, 0:256], 0.0, [r("d64"), r("lt4")], [r("ac4")]),
            "R16": lambda: cp(T.r16[:, 0:4], T.ac4[:, 63:256:64], [r("ac4")], [r("r16")]),
            "cr": lambda: cp(T[crow][:, 0:256], T.rr[:, 0:128].indirect(T.kw[:, 0:16]), [r("rr"), r("kw")], [r(crow)]),
            "Cr": lambda: act(T[crow][:, 0:256], T.rr[:, 0:128].indirect(T.kw[:, 0:16]), F.Copy, [r("rr"), r("kw")], [r(crow)]),
            "cw": lambda: as_list(crow, "cw", 0.125),
            "rm": lambda: cp(T.rm[:, 0:128:2], T.m4t[:, 0:64].indirect(T.r16[:, 0:4]), [r("m4t"), r("r16")], [r("rm")]),
            "cm4": lambda: copy("v", T.cm4[:, 0:256], T.rm[:, 0:128].indirect(T.kw[:, 0:16]), [r("rm"), r("kw")], [r("cm4")]),
            "Cm4": lambda: copy("s", T.cm4[:, 0:256], T.rm[:, 0:128].indirect(T.kw[:, 0:16]), [r("rm"), r("kw")], [r("cm4")]),
            "cm16": prekeys_own,
            "Cm16": lambda: prekeys_own("s"),
            "Rr": lambda: act(T.rr[:, 0:128:2], T.half[:, 0:64].indirect(T.r16[:, 0:4]), F.Copy, [r("half"), r("r16")], [r("rr")], bias=-0.5),
            "Rm": lambda: copy("s", T.rm[:, 0:128:2], T.m4t[:, 0:64].indirect(T.r16[:, 0:4]), [r("m4t"), r("r16")], [r("rm")]),
            "pk": prekeys_next,
        }
        for k in "fso":
            steps[">" + k] = lambda k=k: send_list(k)
        for i in range(4):
            steps["r%d" % i] = lambda i=i: rank_of_key(i)
            steps["g%d" % i] = lambda i=i: first(i, "s")
            steps["v%d" % i] = lambda i=i: first(i, "v")
            steps["m%d" % i] = lambda i=i: mean(i)
            steps["z%d" % i] = lambda i=i: final(i)
            steps["o%d" % i] = lambda i=i: own(i)
        skip = () if t < R - 1 else ("rm", "cm4", "cm16", "pk")
        run(MEANS, steps, skip)
        quant("zc", "zp", "zt", 0, 128)
        for b in range(4):
            mm(b, "pw", 128, "wq", "wp", 128 * b, "zc", "zp", 0)
        for b in range(4):
            o, i, rd, wr = T.ht[:, b:256:4], T.pw[:, 512 * b:512 * b + 64], [bank("pw", b)], [("ht", 64 * b, 64 * b + 64)]
            if b in VRELU:
                ts(o, i, 0.0, 0.03125, amax, mult, rd, wr)
            else:
                act(o, i, F.Relu, rd, wr, scale=0.03125)
        quant("hq%d" % t, "hs%d" % t, "ht", 0, 128)
        land = 128
        send("ha%d" % t, frm, "hc", land, "hq%d" % t, 0, K)
        send("ha%d" % t, frm, "hp", land, "hs%d" % t, 0, K)
        arrival("ha%d" % t, to, 2, [r("hc", land, land + K), r("hp", land, land + K)])
        if t == 0:
            need("y", [r("zc")], [])
            dma("y", "dv", T.vt[:], T.v[:], [], [r("vt")])
        run(AFTER, steps, skip)
        if t == R - 1:
            dma("y", "dol", T.ol[:], T.cf[0:128:16, 0:256], [r("cf")], [])
            quant("qv", "sv", "vt", 0, 128)
        new = "t%d" % (t + 1)
        for b in range(4):
            mm(min(b, 2), "pw", 128, "eq", "esc", 128 * b, "hc", "hp", land - 64 * (b == 3), b != 3, b != 2)


        def came_h(b, on):
            n = 128 if b == 2 else 64
            copy(on, T.dh[:, 64 * b:64 * b + n], T.pw[:, 512 * b:512 * b + n], [bank("pw", b)], [r("dh", 64 * b, 64 * b + n)])

        def picked(b, h):
            o = C * (b - 2) + 128 * h
            act(T.g2[:, o:o + 128], T.dh[:, 64 * b:64 * b + 64].indirect(T.cw[:, 8 * h:8 * h + 8]), F.Copy,
                [r("dh", 64 * b, 64 * b + 64), r("cw")], [r("g2", o, o + 128)])

        def both(b, a=0, e=2):
            a, e = 128 * a, 128 * e
            tt(T[new][:, 4 * a + b:4 * e:4], T.dh[:, 64 * b:64 * b + 64].indirect(T.cw[:, a // 16:e // 16]), T.fo[:, C * b + a:C * b + e], add,
               [r("dh", 64 * b, 64 * b + 64), r("cw"), r("fo", C * b + a, C * b + e)], [(new, C * b + a, C * b + e)])

        def added(b, h):
            o, p, w = C * (b - 2) + 128 * h, 512 * b + 128 * h, C * b + 128 * h
            tt(T[new][:, 512 * h + b:512 * h + 512:4], T.g2[:, o:o + 128], T.pf[:, p:p + 128], add,
               [r("g2", o, o + 128), bank("pf", b)], [(new, w, w + 128)])
        steps = {"d": lambda b: came_h(b, "v"), "D": lambda b: came_h(b, "s"), "G": picked, "b": both, "a": added,
                 "q": lambda h: quant("q%d" % (t + 1), "s%d" % (t + 1), new, 128 * h, 128, 128 * h)}
        run(EXPAND, steps)

    def store_scales(qu, k):
        dma(qu, "ds%d" % k, T.osc[4 * k:4 * k + 4, 0:256], T.s3[32 * k:32 * k + 4, 0:256], [r("s3")], [])
    for h in range(2):
        dma("y", "doc%d" % h, T.oc[:, 512 * h:512 * h + 512], T.q3[:, 128 * h:128 * h + 128].bitcast(dt.uint8), [r("q3", 128 * h, 128 * h + 128)], [])
        mm(h, "pw", 128, "qv", "sv", 0, "q3", "s3", 128 * h)
    act(T.yo[:, 0:128], T.pw[:, 0:128], F.Copy, [bank("pw", 0)], [r("yo", 0, 128)])
    dma("s", "dy0", T.y[:, 0:128], T.yo[:, 0:128], [r("yo", 0, 128)], [])
    cp(T.yo[:, 128:256], T.pw[:, 512:640], [bank("pw", 1)], [r("yo", 128, 256)])
    store_scales("y", 0)
    store_scales("y", 1)
    store_scales("s", 2)
    dma("s", "dy1", T.y[:, 128:256], T.yo[:, 128:256], [r("yo", 128, 256)], [])
    store_scales("y", 3)
    for sname in ("cv", "cs", "ct", "cg", "left"):
        g.sync.wait_ge(T.sem[sname], count[sname])
    for sname in DMAS:
        if known["y"].get(sname, 0) < 16:
            g.sync.wait_ge(T.sem[sname], 16)
